import numpy as np, ml_dtypes
CORES = [40,64,80,88,96,104,120,144]
N = 8
BF = ml_dtypes.bfloat16
def gentries(a):
    return np.ascontiguousarray(a.reshape(8, 16, -1).transpose(0, 2, 1)).reshape(8, -1)
def gtable(e):
    e = np.asarray(e); return np.ascontiguousarray(e.reshape(8, -1, 16).transpose(0, 2, 1)).reshape(128, -1).astype(np.int32)
M, FAR, S, F, RO = 2048, 2, 256, 1024, 6
def trees(rng, top, share):
    on = ((np.arange(M) < top) | (rng.random((N, 8, M)) < share)).astype(np.int64)
    c = np.add.accumulate(on, axis=2) - 1; inner = (on == 1) & (2 * c + 2 <= M - 1)
    pi = np.concatenate([np.zeros((N, 8, 1), np.int64), 1 + np.argsort(rng.random((N, 8, M - 1)), axis=2)], axis=2)
    kl = np.zeros((N, 8, M), np.int64); kr = np.zeros((N, 8, M), np.int64)
    np.put_along_axis(kl, pi, np.where(inner, np.take_along_axis(pi, np.minimum(2 * c + 1, M - 1), 2), 0), 2)
    np.put_along_axis(kr, pi, np.where(inner, np.take_along_axis(pi, np.minimum(2 * c + 2, M - 1), 2), 0), 2)
    return kl, kr, pi
def starts(rng, pi, ia, ib):
    far = np.stack([np.concatenate([d * M + pi[(q + 1 + d) % N] for d in range(FAR)], axis=1) for q in range(N)])
    return np.take_along_axis(pi, ia, 2), np.take_along_axis(far, rng.integers(0, FAR, (N, 8, S)) * M + ib, 2)
def near(rng):
    return (M * rng.random((N, 8, S)) ** 3).astype(np.int64)
def signs(rng, v):
    q = rng.choice(np.array([0.004, 0.015, 0.03, 0.05]), (N, 8, 1, 1))
    return np.where(rng.random(v.shape) < 2 * q * rng.random((N, 8, 1, M)), -v, v)
def parts(rng):
    kl, kr, pi = trees(rng, M // 8, 0.75); a, b = starts(rng, pi, near(rng), near(rng))
    return signs(rng, rng.integers(0, 4097, (N, 8, 16, M))), kl, kr, pi, a, b
def pack(h, kl, kr, a, b):
    return {"h": np.ascontiguousarray(h.reshape(N, 128, M)).astype(np.float32).astype(BF), "kl": kl.astype(np.int32), "kr": kr.astype(np.int32),
            "sa": np.stack([gtable(x) for x in a]), "sb": np.stack([gtable(x) for x in b])}
def setup_inputs(rng):
    h, kl, kr, pi, a, b = parts(rng)
    return pack(h, kl, kr, a, b)
def setup_inputs_alike(rng):
    h, kl, kr, pi, a, b = parts(rng)
    a[:, 0] = np.tile(a[:, 0, :4], (1, S // 4)); b[:, 0] = np.tile(b[:, 0, :4], (1, S // 4))
    a[:, 1] = rng.choice(np.array([0, M - 1]), (N, S)); b[:, 1] = rng.choice(np.array([0, FAR * M - 1]), (N, S))
    a[:, 1, 0] = 0; b[:, 1, 0] = 0; kl[:, 1, 0] = 0; kr[:, 1, 0] = 0; h[:, 1, :, 0] = np.abs(h[:, 1, :, 0])
    la, lb = starts(rng, pi, M - 1 - rng.integers(0, M // 8, (N, 8, S)), M - 1 - rng.integers(0, M // 8, (N, 8, S)))
    a[:, 2] = la[:, 2]; b[:, 2] = lb[:, 2]
    inner = kl > 0; own = np.maximum(np.arange(M), 1)
    kl[:, 4] = np.where(inner[:, 4], own, 0); kr[:, 4] = np.where(inner[:, 4], own, 0)
    few = np.array([1, M // 2, M - 1])
    kl[:, 6] = np.where(inner[:, 6], rng.choice(few, (N, M)), 0); kr[:, 6] = np.where(inner[:, 6], rng.choice(few, (N, M)), 0)
    return pack(h, kl, kr, a, b)
def setup_inputs_cold(rng):
    h, kl, kr, pi, a, b = parts(rng); o = [int(x) for x in rng.permutation(8)]
    h[:, o[0]] = -1 - np.abs(h[:, o[0]])
    h[:, o[1]] = np.where(rng.random((N, 16, M)) < 0.1, -1, 1) * np.abs(h[:, o[1]])
    for g in (o[2], o[4], o[5]):
        h[:, g] = np.abs(h[:, g]); z = pi[:, g, M - 1]
        h[np.arange(N), g, 0, z] = -65536; a[:, g] = z[:, None]
    one = np.array([7, 9, 10, 11, 12, 13, 14]); level = np.arange(31, 63)
    for q in range(N):
        nx = (q + 1) % N
        h[q, o[4], 0, pi[q, o[4], one]] = -65536; h[q, o[5], 0, pi[q, o[5], level]] = -65536
        j = (0, S - 1)[q % 2]; a[q, o[2], j] = pi[q, o[2], 1]; b[q, o[2], j] = pi[nx, o[2], 1]
        j = (0, S - 1, S // 2, 17)[q % 4]
        a[q, o[4], j] = pi[q, o[4], M - 3]; b[q, o[4], j] = pi[nx, o[4], (M - 3, 1)[q % 2]]
        a[q, o[5], j] = pi[q, o[5], M - 3]; b[q, o[5], j] = pi[nx, o[5], (7, 3, 1, 0)[q % 4]]
    q = int(rng.integers(0, N)); h[q, o[3]] = -1 - np.abs(h[q, o[3]])
    return pack(h, kl, kr, a, b)
def setup_inputs_room(rng):
    kl, kr, pi = trees(rng, M, 1.0); h = rng.integers(0, 4097, (N, 8, 16, M))
    h[np.arange(N)[:, None], np.arange(8)[None, :], rng.integers(0, 16, (N, 8)), pi[:, :, M - 1]] = -65536
    ia = near(rng); ib = near(rng); w = S // 8; o = rng.permutation(8); low = M // 2 - 1; safe = low + M // 16
    for q in range(N):
        for g in range(8):
            c = int(o[g])
            if c == 7: continue
            leaf = rng.integers(low, M - 1, S); deep = rng.integers(0, M // 8 - 1, S)
            if c < 3: deep = rng.integers(M // 16 - 1, M // 8 - 1, S)
            if c == 4 or c == 5:
                t = M // 16 if c == 4 else M // 32
                deep = rng.integers(t - 1, 2 * t - 1, S); leaf = rng.integers(low, safe, S)
                dead = safe + np.flatnonzero(rng.random(M - 1 - safe) < 0.75)
                h[q, g, rng.integers(0, 16, len(dead)), pi[q, g, dead]] = -65536
            u = deep
            if c < 4:
                n = 3 * S + w + (0, 1, -1, (0, 1, -1)[q % 3])[c]; x = n // 7; y = n - 7 * x
                u = np.concatenate([deep[:x], rng.integers(M // 4 - 1, M // 2 - 1, y), np.full(w, M - 1, np.int64), rng.integers(M // 2 - 1, M - 1, S - x - y - w)])
                u = rng.permutation(u)
            flip = rng.random(S) < 0.5
            ia[q, g] = np.where(flip, leaf, u); ib[q, g] = np.where(flip, u, leaf)
    a, b = starts(rng, pi, ia, ib)
    return pack(h, kl, kr, a, b)
def setup_inputs_spread(rng):
    kl, kr, pi = trees(rng, 32, 0.55); a, b = starts(rng, pi, near(rng), near(rng))
    v = np.floor(np.exp2(16 * rng.random((N, 8, 1, M))) * rng.random((N, 8, 16, M))).astype(np.int64)
    v = np.where(rng.random(v.shape) < 0.01, 65536, v)
    return pack(signs(rng, v), kl, kr, a, b)
def setup_inputs_ties(rng):
    h, kl, kr, pi, a, b = parts(rng)
    u = rng.random((N, 8, 16, M)); h = np.where(u < 0.05, -1, np.where(u < 0.15, 0, 1)) * np.array([1, 128, 32768, 65536, 1, 2, 1, 4]).reshape(1, 8, 1, 1)
    h[:, 6, :8] = 65536
    q = np.arange(N); nx = (q + 1) % N
    h[q, 0, :, pi[q, 0, 1]] = -65536
    for j, v in ((3, 1), (4, 1), (M - 1, 1), (2, -2), (5, 0), (6, 0), (9, -1), (M - 2, 4), (M - 3, 4)): h[q, 0, :, pi[q, 0, j]] = v
    kl[q, 0, pi[q, 0, 9]] = pi[q, 0, M - 2]; kr[q, 0, pi[q, 0, 9]] = pi[q, 0, M - 3]
    a[q, 0, 0] = pi[q, 0, M - 1]; b[q, 0, 0] = pi[nx, 0, 1]
    a[q, 0, 1] = pi[q, 0, 1]; b[q, 0, 1] = pi[nx, 0, M - 1]
    a[q, 0, 2] = pi[q, 0, 2]; b[q, 0, 2] = pi[nx, 0, 9]
    d = pack(h, kl, kr, a, b); x = d["h"].astype(np.float32)
    d["h"] = np.where((x == 0) & (rng.random(x.shape) < 0.5), np.float32(-0.0), x).astype(BF)
    return d
def check_inputs(d):
    bad = []
    x = np.asarray(d["h"]).astype(np.float32)
    if not np.all(x == np.floor(x)): bad.append("whole numbers in h")
    if not np.max(np.abs(x)) <= 65536: bad.append("range of h")
    for k, hi in (("kl", M - 1), ("kr", M - 1), ("sa", M - 1), ("sb", FAR * M - 1)):
        if np.min(d[k]) < 0 or np.max(d[k]) > hi: bad.append("range of " + k)
    if not np.all((np.asarray(d["kl"]) == 0) == (np.asarray(d["kr"]) == 0)): bad.append("two kids or none")
    return bad
def reference(h, kl, kr, sa, sb):
    hw = h.astype(np.float32).astype(np.int64).reshape(N, 8, 16, M); left = kl.astype(np.int64); right = kr.astype(np.int64)
    ya = np.full((N, 8, F), -1.0, np.float32); yb = np.full((N, 8, F), -1.0, np.float32); ys = np.zeros((N, 8, F), np.float32)
    swap = np.arange(16) ^ 1
    for r in range(N):
        far = [(r + 1 + d) % N for d in range(FAR)]; first = gentries(sa[r]).astype(np.int64); second = gentries(sb[r]).astype(np.int64)
        for g in range(8):
            ha = hw[r, g]; hb = np.concatenate([hw[q, g] for q in far], axis=1); hs = hb[swap]
            la, ra = left[r, g], right[r, g]
            lb = np.concatenate([np.where(left[q, g] > 0, left[q, g] + d * M, 0) for d, q in enumerate(far)])
            rb = np.concatenate([np.where(right[q, g] > 0, right[q, g] + d * M, 0) for d, q in enumerate(far)])
            za = np.add.reduce(ha, axis=0); zb = np.add.reduce(hb, axis=0)
            a, b = first[g], second[g]
            for rnd in range(RO):
                fa = la[a] == 0; fb = lb[b] == 0
                oa = ~fa & (fb | (za[a] >= zb[b])); ob = ~fb & ~oa
                ca = np.stack([np.where(oa, la[a], a), np.where(oa, ra[a], a)], axis=1).reshape(-1)
                cb = np.stack([np.where(ob, lb[b], b), np.where(ob, rb[b], b)], axis=1).reshape(-1)
                there = np.stack([np.ones(len(a), bool), oa | ob], axis=1).reshape(-1)
                keep = there & np.all(ha[:, ca] + hs[:, cb] >= 0, axis=0)
                a = ca[keep][:F]; b = cb[keep][:F]
            ya[r, g, :len(a)] = a; yb[r, g, :len(a)] = b; ys[r, g, :len(a)] = za[a] + zb[b]
    return {"ya": ya, "yb": yb, "ys": ys}

@@ -1,0 +1,565 @@
+from concourse.bass import DstId, RemoteDMATransfer
+from concourse.mybir import AluOpType as A, ActivationFunctionType as AF
+
+M_, FAR, F_ = 2048, 2, 1024
+PAD, OWN, TW = 4096, 4112, 6160
+WW = 5128
+KX = 112 + 64 * 3
+OPT = {"hra": 1, "f": [2, 0, 2, 2, 4, 6, 3, 2, 1, 3, 2], "cuts": [0, 8, 24, 44, 64], "mc": 640, "fc": [0, 7, 13, 16]}
+
+SCRATCH = {}
+for _n, _c, _d in (
+        ("hs", [M_], "bfloat16"), ("HL HR", [TW], "bfloat16"), ("H", [TW + 16], "bfloat16"), ("IX", [TW], "float32"),
+        ("IU UR", [TW + 16], "float32"), ("G", [4096], "float32"),
+        ("GU", [1024], "float32"), ("nU VL VR", [1792], "bfloat16"), ("Mb Mc mk", [1024], "bfloat16"),
+        ("win0 win1 win2 win3", [WW], "bfloat16"), ("KL KR vI Wi", [128], "int32"), ("SA SB", [16], "int32"),
+        ("kin ti tj tf tg Po Pf", [256], "float32"), ("lin lsend", [512], "uint16"), ("lown", [256], "uint16"),
+        ("ksend kown ui uh vf uf ug lf lb ls r0", [128], "float32"), ("XO UO", [KX], "uint16"), ("AB", [32], "uint16"),
+        ("off", [64], "uint16"), ("FA", [128], "uint16"), ("pI ci cj", [4], "int32"), ("xI", [256], "int32"),
+        ("jI Ci ai bi", [64], "int32"), ("cf cq oe oer ov c256 w1 w0", [4], "float32"), ("cc", [16], "float32"),
+        ("CB", [24], "float32"), ("B1 B2 B3 BK WL WE WP WC WN WP0 WC0 WN0", [144], "bfloat16"),
+        ("Blk ML MR Tri Idn PM0 PM1", [128], "bfloat16"),
+        ("J0 JC JD Z0 O2 d3 tU tX zU zX b4 Xf Uf T1 T2 O df al oa ob oz", [64], "float32"), ("P2", [8, 16], "float32"),
+        ("TI TO", [8, 32], "float32"), ("LR", [2, 128], "int32"), ("kk", [2, 64], "bfloat16"),
+        ("S", [72], "float32"), ("dead", [64], "bfloat16"), ("d2", [32], "bfloat16")):
+    for _x in _n.split():
+        SCRATCH[_x] = ("sbuf", [128] + _c, _d)
+SCRATCH.update({"pc": ("psum", [128, 2, 512], "float32"), "pm": ("psum", [128, 2, 512], "float32"),
+                "pv": ("psum", [128, 512], "float32"), "pw": ("psum", [128, 512], "float32"),
+                "pb": ("psum", [128, 512], "float32"), "pt": ("psum", [128, 512], "float32")})
+SEMAPHORES = ["sv", "sa_", "sp", "sg", "lhs", "lkl", "lkr", "lsa", "lsb", "lsw", "kown", "kowr", "kfu", "kfr", "outs",
+              "sent", "arrh", "arri", "farh", "fari"]
+
+
+def helpers_of(T, topo, q):
+    n = len(T.cores)
+    src = T.cores[q]
+    dsts = [T.cores[(q - d) % n] for d in range(1, FAR + 1)]
+    ok = [c for c in topo.cores_of(src) if c != src and all(topo.may_write(c, x) for x in dsts)]
+    near = [c for c in ok if topo.die(c) == topo.die(src)]
+    other = [c for c in ok if topo.die(c) != topo.die(src)]
+    return near[:2] + other[:2], dsts
+
+
+def bits(engs):
+    m = 0
+    for e in engs:
+        m |= 1 << e
+    return m
+
+
+def dst_id(topo, dst, src):
+    rid, pid = topo.addr(dst, src)
+    return DstId(rid=rid, pnc=pid)
+
+
+def info_helper(hs_, d):
+    return hs_[(2 * d) % len(hs_)]
+
+
+def helper_program(g, core, T, topo):
+    for q in range(len(T.cores)):
+        hs_, dsts = helpers_of(T, topo, q)
+        if core not in hs_:
+            continue
+        i = hs_.index(core)
+        w = M_ // len(hs_)
+        sent = 0
+        for d, x in enumerate(dsts):
+            if topo.may_write(T.cores[q], x) or info_helper(hs_, d) != core:
+                continue
+            g.wait_ge(T.sem.arri, 8)
+            e = topo.engines(core, x)
+            ks, ls = T.kin[:, 128 * d:128 * d + 128], T.lin[:, 256 * d:256 * d + 256]
+            g.remote_dma_fused([
+                RemoteDMATransfer(dst_ids=[dst_id(topo, x, core)], dma_engine_mask=bits(e[0:4]), remote_sem=T.sem.fari, src=ks, dst=ks),
+                RemoteDMATransfer(dst_ids=[dst_id(topo, x, core)], dma_engine_mask=bits(e[4:8]), remote_sem=T.sem.fari, src=ls, dst=ls),
+            ], local_sem=T.sem.sent)
+            sent += 8
+        g.wait_ge(T.sem.arrh, 4)
+        tr = []
+        for d, x in enumerate(dsts):
+            e = topo.engines(core, x)
+            c0 = d * M_ + i * w
+            tr.append(RemoteDMATransfer(dst_ids=[dst_id(topo, x, core)], dma_engine_mask=bits(e[4 * d:4 * d + 4]),
+                                        remote_sem=T.sem.farh, src=T.HL[:, 0:w], dst=T.H[:, c0:c0 + w]))
+        g.remote_dma_fused(tr, local_sem=T.sem.sent)
+        sent += 4 * len(dsts)
+        g.wait_ge(T.sem.sent, sent)
+
+
+def rank_program(g, core, T, topo):
+    rank = T.rank_of(core)
+    if rank is None:
+        helper_program(g, core, T, topo)
+        return
+    Q = {"v": g.vector, "a": g.scalar, "p": g.tensor, "g": g, "s": g.sync}
+    esem = {"v": "sv", "a": "sa_", "p": "sp", "g": "sg"}
+    total = {}
+    seen = {k: {} for k in Q}
+    wr, rd = {}, {}
+
+    def wait(q, tok):
+        s, n = tok
+        if n is None:
+            n = total[s]
+        if q == "p" and s == "sp":
+            return
+        if seen[q].get(s, 0) < n:
+            Q[q].wait_ge(T.sem[s], n)
+            seen[q][s] = n
+
+    def before(q, R, W):
+        for k in list(R) + list(W):
+            if k in wr:
+                wait(q, wr[k])
+        for k in W:
+            for t in rd.get(k, []):
+                wait(q, t)
+        for k in R:
+            if k.startswith("p:"):
+                for t in rd.get(k, []):
+                    if t[0] != esem.get(q):
+                        wait(q, t)
+
+    def after(tok, R, W):
+        for k in R:
+            rd.setdefault(k, []).append(tok)
+        for k in W:
+            wr[k] = tok
+            rd[k] = []
+
+    def op(q, fn, R, W):
+        before(q, R, W)
+        s = esem[q]
+        fn().then_inc(T.sem[s], 1)
+        total[s] = total.get(s, 0) + 1
+        after((s, total[s]), R, W)
+
+    def dma(q, out, in_, s, R, W):
+        before(q, R, W)
+        Q[q].dma_start(out, in_).then_inc(T.sem[s], 16)
+        total[s] = total.get(s, 0) + 16
+        after((s, None), R, W)
+
+    def mm(items, R, W, start=True, stop=True):
+        before("p", R, W)
+        for i, (o, l, r) in enumerate(items):
+            ins = g.tensor.matmul(o, l, r, start and i == 0, stop and i == len(items) - 1)
+        ins.then_inc(T.sem.sp, 1)
+        total["sp"] = total.get("sp", 0) + 1
+        after(("sp", total["sp"]), R, W)
+
+    V = g.vector
+
+    def ts(out, in0, s1, s2, o0, o1, R, W):
+        if s2 is None:
+            op("v", lambda: V.tensor_scalar(out, in0, s1, None, o0), R, W)
+        else:
+            op("v", lambda: V.tensor_scalar(out, in0, s1, s2, o0, o1), R, W)
+
+    def tt(out, a, b, o, R, W):
+        op("v", lambda: V.tensor_tensor(out, a, b, o), R, W)
+
+    def cp(out, a, R, W):
+        op("v", lambda: V.tensor_copy(out, a), R, W)
+
+    def ms(out, c, W):
+        op("v", lambda: V.memset(out, c), [], W)
+
+    def act(out, in_, f, R, W, **kw):
+        op("a", lambda: g.scalar.activation(out, in_, f, **kw), R, W)
+
+    def fiota(name, pat, base):
+        op("g", lambda: g.iota(T[name][:], pat, base, 0, allow_small_or_imprecise_dtypes=True), [], [name])
+
+    def sel(W_, s):
+        return W_[:, 15 - s:143 - s]
+
+    AND, SHR, EQ, MUL, ADD = A.bitwise_and, A.logical_shift_right, A.is_equal, A.mult, A.add
+    hs_, dsts = helpers_of(T, topo, rank)
+
+    dma("s", T.KL[:], T.kl[:], "lkl", [], ["KL"])
+    dma("a", T.KR[:], T.kr[:], "lkr", [], ["KR"])
+    dma("s", T.hs[:], T.h[:], "lhs", [], ["hs"])
+    dma("s", T.H[0::2, OWN:TW], T.h[1::2, :], "lsw", [], ["Ho0"])
+    dma("s", T.H[1::2, OWN:TW], T.h[0::2, :], "lsw", [], ["Ho1"])
+    dma("s", T.SA[:], T.sa[:], "lsa", [], ["SA"])
+    dma("s", T.SB[:], T.sb[:], "lsb", [], ["SB"])
+
+    op("g", lambda: g.iota(T.pI[:, 0:1], [[0, 1]], 0, 1), [], ["pI"])
+    op("g", lambda: g.iota(T.xI[:], [[1, 256]], 0, 0), [], ["xI"])
+    op("g", lambda: g.iota(T.vI[:], [[1, 128]], 0, 128), [], ["vI"])
+    fiota("ti", [[0, 8], [8, 32]], 0)
+    fiota("tj", [[1, 8], [0, 32]], 0)
+    op("g", lambda: g.iota(T.jI[:], [[1, 64]], 0, 64), [], ["jI"])
+    fiota("ui", [[1, 8], [0, 16]], 0)
+    fiota("uf", [[0, 16], [2, 2], [0, 4]], -1)
+    fiota("ug", [[0, 8], [-17, 4], [0, 4]], 0)
+    fiota("uh", [[1, 64], [0, 2]], 0)
+    fiota("JC", [[16, 64]], 0)
+    p = T.pI[:, 0:1]
+    ms(T.c256[:], 256.0, ["c256"])
+    ms(T.H[:, PAD:OWN], -262144.0, ["Hp"])
+    ts(T.ci[:, 0:1], p, 3, None, AND, None, ["pI"], ["ci0"])
+    ts(T.ci[:, 1:2], p, 2, 3, SHR, AND, ["pI"], ["ci1"])
+    ts(T.ci[:, 2:3], p, 4, None, SHR, None, ["pI"], ["ci2"])
+    ts(T.ci[:, 3:4], p, 4, 1, SHR, AND, ["pI"], ["ci3"])
+    ms(T.S[:, 0:1], 0.0, ["S0"])
+    cp(T.cf[:], T.ci[:], ["ci0", "ci1", "ci2", "ci3"], ["cf"])
+    for name in ("IU", "UR", "HL", "HR", "IX"):
+        ms(T[name][:, PAD:OWN], 0.0, [name + "p"])
+    ce, cv, cg, ch = (T.cf[:, i:i + 1] for i in range(4))
+    c15, cmR, chi, csg, ch0, cpf, cbm, c2, c3, cnz, cpm = (T.cc[:, i:i + 1] for i in range(11))
+    act(csg, cv, AF.Sigmoid, ["cf"], ["csg"], bias=384.0, scale=-256.0)
+    ts(T.oe[:], T.xI[:, 0:4], ce, None, EQ, None, ["xI", "cf"], ["oe"])
+    ts(T.ov[:], T.xI[:, 0:4], cv, None, EQ, None, ["xI", "cf"], ["ov"])
+    e0, e1, e2, e3 = (T.oe[:, i:i + 1] for i in range(4))
+    v0, v1, v2, v3 = (T.ov[:, i:i + 1] for i in range(4))
+    ts(T.Po[:], T.xI[:], e0, None, MUL, None, ["xI", "oe"], ["Po"])
+    ts(T.CB[:, 16:24], T.xI[:, 0:8], e1, None, MUL, None, ["xI", "oe"], ["CBo"])
+    ts(c15, cg, 16.0, 15.0, MUL, ADD, ["cf"], ["c15"])
+    ts(ch0, ch, -1.0, 1.0, MUL, ADD, ["cf"], ["ch0"])
+    ts(cmR, v0, -1.0, 1.0, MUL, ADD, ["ov"], ["cmR"])
+    ts(T.B1[:], T.xI[:, 0:144], c15, None, EQ, None, ["xI", "c15"], ["B1"])
+    ts(T.vI[:], T.vI[:], M_ - 1, None, AND, None, ["vI"], ["vI"])
+    ts(T.CB[:, 0:16], T.xI[:, 0:16], 8.0, e2, MUL, MUL, ["xI", "oe"], ["CBf"])
+    ts(T.vf[:], T.vI[:], float(2 ** 22), None, ADD, None, ["vI"], ["vf"])
+    ms(T.H[:, TW:TW + 16], -262144.0, ["Hq"])
+    ms(T.IU[:, TW:TW + 16], 0.0, ["IUq"])
+    ms(T.UR[:, TW:TW + 16], 0.0, ["URq"])
+    ts(T.tf[:], T.ti[:], e1, None, MUL, None, ["ti", "oe"], ["tf"])
+    ts(T.lf[:], T.KL[:], 0.0, None, EQ, None, ["KL"], ["lf"])
+    ts(T.r0[:], T.KR[:], 2048.0, None, MUL, None, ["KR"], ["r0"])
+    ts(T.tg[:], T.tj[:], e2, None, MUL, None, ["tj", "oe"], ["tg"])
+    tt(T.ls[:], T.lf[:], T.vf[:], MUL, ["lf", "vf"], ["ls"])
+    tt(T.Pf[:], T.tf[:], T.tg[:], ADD, ["tf", "tg"], ["Pf"])
+
+    def blk(b):
+        return (256 * b, T.Pf, "Pf", "CBf") if b < 16 else (OWN + 256 * (b - 16), T.Po, "Po", "CBo")
+
+    def iu_blk(b):
+        c, P_, k1, k2 = blk(b)
+        act(T.IU[:, c:c + 256], P_[:], AF.Identity, [k1, k2], ["IU%d" % b], bias=T.CB[:, b:b + 1])
+
+    def ur_blk(b):
+        c, P_, k1, k2 = blk(b)
+        ts(T.UR[:, c:c + 256], P_[:], T.CB[:, b:b + 1], cmR, ADD, MUL, [k1, k2, "cmR"], ["UR%d" % b])
+
+    for b in list(range(16, 24)) + list(range(16)):
+        iu_blk(b)
+    IUF, IUO = ["IU%d" % b for b in range(16)], ["IU%d" % b for b in range(16, 24)]
+    URF, URO = ["UR%d" % b for b in range(16)], ["UR%d" % b for b in range(16, 24)]
+
+    tt(T.r0[:], T.r0[:], T.KL[:], ADD, ["r0", "KL"], ["r0"])
+    mm([(T.pv[:, 0:128], sel(T.B1, s), T.hs[:, 128 * s:128 * s + 128]) for s in range(16)], ["B1", "hs"], ["p:v"])
+    ts(T.lb[:], T.lf[:], float(2 ** 22), None, MUL, None, ["lf"], ["lb"])
+    tt(T.P2[:], T.r0[:], T.ls[:], ADD, ["r0", "ls"], ["P2a"])
+    ts(T.TI[:, :, 0:16], T.P2[:], ch0, None, MUL, None, ["P2a", "ch0"], ["TI0"])
+    ts(T.TI[:, :, 16:32], T.P2[:], ch, None, MUL, None, ["P2a", "cf"], ["TI1"])
+    op("v", lambda: V.transpose(T.TO[:], T.TI[:]), ["TI0", "TI1"], ["TO"])
+    for c in range(8):
+        tt(T.Wi[:, c:128:8], T.TO[:, c, 0:16], T.TO[:, c, 16:32], ADD, ["TO"], ["Wi%d" % c])
+    WI = ["Wi%d" % c for c in range(8)]
+    Li, Ri = T.LR[:, 0, :], T.LR[:, 1, :]
+    ts(Ri, T.Wi[:], 11, None, SHR, None, WI, ["Ri"])
+    ts(Li, T.Wi[:], M_ - 1, None, AND, None, WI, ["Li"])
+    ts(T.r0[:], Ri, float(M_), float(M_), A.is_ge, MUL, ["Ri"], ["r0"])
+    cp(T.lown[:], T.LR[:], ["Li", "Ri"], ["loL", "loR"])
+    tt(T.r0[:], T.r0[:], Ri, ADD, ["r0", "Ri"], ["r0"])
+    ts(T.lsend[:, 256:512], T.LR[:], float(M_), None, ADD, None, ["Li", "Ri"], ["ls1L", "ls1R"])
+    cp(T.lsend[:, 128:256], T.r0[:], ["r0"], ["ls0R"])
+    cp(T.lsend[:, 0:128], Li, ["Li"], ["ls0L"])
+    tt(T.ksend[:], T.lb[:], T.pv[:, 0:128], A.subtract, ["lb", "p:v"], ["ksend"])
+    ts(T.kown[:], T.ksend[:], -1.0, 0.5, MUL, ADD, ["ksend"], ["kown"])
+
+    before("g", ["ksend", "ls0L", "ls0R", "ls1L", "ls1R"], [])
+    used, tr = set(), []
+    for d in sorted(range(FAR), key=lambda d: not topo.may_write(core, dsts[d])):
+        direct = topo.may_write(core, dsts[d])
+        x = dsts[d] if direct else info_helper(hs_, d)
+        for src, dst in ((T.ksend[:], T.kin[:, 128 * d:128 * d + 128]), (T.lsend[:, 256 * d:256 * d + 256], T.lin[:, 256 * d:256 * d + 256])):
+            e = [y for y in topo.engines(core, x) if y not in used][:4]
+            used.update(e)
+            tr.append(RemoteDMATransfer(dst_ids=[dst_id(topo, x, core)], dma_engine_mask=bits(e),
+                                        remote_sem=T.sem.fari if direct else T.sem.arri, src=src, dst=dst))
+    g.remote_dma_fused(tr, local_sem=T.sem.sent)
+
+    before("g", ["hs"], [])
+    w = M_ // len(hs_)
+    g.remote_dma_fused([RemoteDMATransfer(dst_ids=[dst_id(topo, c, core)], dma_engine_mask=bits(topo.engines(core, c)[4 * i:4 * i + 4]),
+                                          remote_sem=T.sem.arrh, src=T.hs[:, i * w:(i + 1) * w], dst=T.HL[:, 0:w])
+                        for i, c in enumerate(hs_)], local_sem=T.sem.sent)
+    total["sent"] = 16 + 4 * len(hs_)
+    total["farh"], total["fari"] = 4 * FAR * len(hs_), 8 * FAR
+    wr["Hf"], wr["kin"], wr["lin"] = ("farh", None), ("fari", None), ("fari", None)
+    wins = [T.win0, T.win1, T.win2, T.win3]
+
+    before("s", ["kown"], IUO)
+    for f in (3, 7, 11):
+        dma("s", T.IU[f::16, OWN:TW], T.kown[:], "kown", ["kown"], ["IUok%d" % f])
+    for b in range(16, 24):
+        ur_blk(b)
+    before("s", [], URO)
+    for f in (7, 11):
+        dma("s", T.UR[f::16, OWN:TW], T.kown[:], "kowr", ["kown"], ["URok%d" % f])
+    IUO = IUO + ["IUok3", "IUok7", "IUok11", "IUp", "IUq"]
+    URO = URO + ["URok7", "URok11", "URq"]
+    for b in range(16):
+        ur_blk(b)
+
+    def kidb(q, dstT, name, lst, win, c0, n, R):
+        if q == "a":
+            act(dstT[:, c0:c0 + n], win.indirect(lst), AF.Copy, R, [name])
+        else:
+            cp(dstT[:, c0:c0 + n], win.indirect(lst), R, [name])
+
+    HO = ["Ho0", "Ho1", "Hp", "Hq"]
+    kidb("a", T.HL, "HLo", T.lown[:, 0:128], T.H[:, OWN:TW + 16], OWN, 2048, HO + ["loL"])
+    kidb("a", T.HR, "HRo", T.lown[:, 128:256], T.H[:, OWN:TW + 16], OWN, 2048, HO + ["loR"])
+
+    def ix_a(lst, lo, hi, gc, n, R):
+        act(T.G[:, gc:gc + n], T.IU[:, lo:hi].indirect(lst), AF.Identity, R + ["ov"], ["G%d" % gc], scale=v0)
+
+    def ix_v(lst, lo, hi, gc, c0, n, R):
+        tt(T.IX[:, c0:c0 + n], T.UR[:, lo:hi].indirect(lst), T.G[:, gc:gc + n], ADD, R + ["G%d" % gc], ["IX%d" % c0])
+
+    for i in range(4):
+        ix_a(T.lown[:, 32 * i:32 * i + 32], OWN, TW + 16, 512 * i, 512, IUO + ["loL"])
+
+    ts(T.oer[:], T.xI[:, 0:4], ce, 3.0, ADD, EQ, ["xI", "cf"], ["oer"])
+    ts(chi, e3, 0.5 - 1e6, 1e6, MUL, ADD, ["oe"], ["chi"])
+    ts(cbm, v1, -256.0, 128.0, MUL, ADD, ["ov"], ["cbm"])
+    cp(cpf, p, ["pI"], ["cpf"])
+    ts(T.jI[:], T.jI[:], F_ - 1, None, AND, None, ["jI"], ["jI"])
+    op("v", lambda: V.tensor_tensor_scan(T.w1[:], T.c256[:], T.oer[:], 0.0, MUL, ADD), ["c256", "oer"], ["w1"])
+    op("v", lambda: V.tensor_tensor_scan(T.w0[:, 1:4], T.c256[:, 1:4], T.oer[:, 1:4], 0.0, MUL, ADD), ["c256", "oer"], ["w0"])
+    ts(T.Blk[:], T.ui[:], cg, None, EQ, None, ["ui", "cf"], ["Blk"])
+    ts(T.Idn[:], T.xI[:, 0:128], cpf, None, EQ, None, ["xI", "cpf"], ["Idn"])
+    cp(T.J0[:], T.jI[:], ["jI"], ["J0"])
+    ts(T.cj[:, 0:1], p, 15, None, AND, None, ["pI"], ["cj0"])
+    ts(T.cj[:, 1:2], p, 7, None, AND, None, ["pI"], ["cj1"])
+    ts(T.cj[:, 2:3], p, 3, 1, SHR, AND, ["pI"], ["cj2"])
+    tt(c2, c15, v2, ADD, ["c15", "ov"], ["c2"])
+    tt(c3, c15, v1, ADD, ["c15", "ov"], ["c3"])
+    cp(T.cq[:, 0:3], T.cj[:, 0:3], ["cj0", "cj1", "cj2"], ["cq"])
+    ts(cnz, v3, -1.0, 1.0, MUL, ADD, ["ov"], ["cnz"])
+    ts(T.B2[:], T.xI[:, 0:144], c2, None, EQ, None, ["xI", "c2"], ["B2"])
+    ts(T.B3[:], T.xI[:, 0:144], c3, None, EQ, None, ["xI", "c3"], ["B3"])
+    ts(cpm, cg, 8.0, T.cq[:, 1:2], MUL, ADD, ["cf", "cq"], ["cpm"])
+    ts(T.cq[:, 3:4], T.cq[:, 2:3], -1.0, 1.0, MUL, ADD, ["cq"], ["cq3"])
+    ts(T.JD[:], T.JC[:], T.cq[:, 0:1], 2048.0, ADD, ADD, ["JC", "cq"], ["JD"])
+    ts(T.JC[:], T.JC[:], T.cq[:, 0:1], None, ADD, None, ["JC", "cq"], ["JC"])
+    ts(T.PM0[:], T.uh[:], cpm, T.cq[:, 3:4], EQ, MUL, ["uh", "cpm", "cq3"], ["PM0"])
+    ts(T.PM1[:], T.uh[:], cpm, T.cq[:, 2:3], EQ, MUL, ["uh", "cpm", "cq"], ["PM1"])
+    ms(T.Z0[:], 0.0, ["Z0"])
+    w1, w0 = T.w1[:, 3:4], T.w0[:, 3:4]
+    for name, B, a_, b_ in (("WL", "B1", w1, v0), ("WE", "B3", w1, csg), ("WP", "B1", w1, v2), ("WC", "B1", w1, csg), ("WN", "B2", w1, cnz),
+                            ("WP0", "B1", w0, v2), ("WC0", "B1", w0, csg), ("WN0", "B2", w0, cnz)):
+        ts(T[name][:], T[B][:], a_, b_, MUL, MUL, [B, "w1", "w0", "ov", "csg", "cnz"], [name])
+    ts(T.BK[:], T.B1[:], 4096.0, None, MUL, None, ["B1"], ["BK"])
+    tt(T.ML[:], T.Blk[:], T.uf[:], MUL, ["Blk", "uf"], ["ML"])
+    tt(T.MR[:], T.Blk[:], T.ug[:], MUL, ["Blk", "ug"], ["MR"])
+    ts(T.AB[:, 0:16], T.SA[:], float(OWN), None, ADD, None, ["SA"], ["A0"])
+    cp(T.AB[:, 16:32], T.SB[:], ["SB"], ["B0"])
+    for i in range(4):
+        ix_v(T.lown[:, 128 + 32 * i:160 + 32 * i], OWN, TW + 16, 512 * i, OWN + 512 * i, 512, URO + ["loR"])
+    for i, wn in enumerate(wins):
+        op("g", lambda: g.iota(wn[:, 0:1026], [[0, 1026]], 0, 0, allow_small_or_imprecise_dtypes=True), [], ["win%d" % i])
+    op("g", lambda: g.affine_select(T.Tri[:], T.Blk[:], [[1, 128]], A.is_gt, 0.0, 0, -1), ["Blk"], ["Tri"])
+
+    before("s", ["kin"], IUF + URF)
+    for tab, keys, rows, s in (("IU", IUF, (3, 7, 11), "kfu"), ("UR", URF, (7, 11), "kfr")):
+        for f in rows:
+            for d in range(FAR):
+                dma("s", T[tab][f::16, M_ * d:M_ * d + M_], T.kin[:, 128 * d:128 * d + 128], s, ["kin"], ["%sk%d_%d" % (tab, d, f)])
+                keys.append("%sk%d_%d" % (tab, d, f))
+    IUA = IUF + IUO
+    IXA = ["IX%d" % c for c in range(0, PAD, 512)] + ["IX%d" % (OWN + 512 * i) for i in range(4)] + ["IXp"]
+    HA = HO + ["Hf"]
+    HLA = ["HLo", "HLp"] + ["HL%d" % i for i in range(8)]
+    HRA = ["HRo", "HRp"] + ["HR%d" % i for i in range(8)]
+
+    def farl(i, right):
+        c = 256 * (i // 4) + 128 * right + 32 * (i % 4)
+        return T.lin[:, c:c + 32]
+
+    def kid(q, i, right):
+        return lambda: kidb(q, T.HR if right else T.HL, ("HR%d" if right else "HL%d") % i, farl(i, right), T.H[:, 0:OWN], 512 * i, 512, ["Hf", "Hp", "lin"])
+
+    hra = OPT["hra"]
+    fill_a = [lambda i=i: ix_a(farl(i, 0), 0, OWN, 512 * i, 512, IUF + ["IUp", "lin"]) for i in range(8)]
+    fill_v = [lambda i=i: ix_v(farl(i, 1), 0, OWN, 512 * i, 512 * i, 512, URF + ["URp", "lin"]) for i in range(8)]
+    fill_a += [kid("a", i, 0) for i in range(8)] + [kid("a", i, 1) for i in range(8 - hra, 8)]
+    fill_v += [kid("v", i, 1) for i in range(8 - hra)]
+
+    def fill(na, nv):
+        for _ in range(na):
+            if fill_a:
+                fill_a.pop(0)()
+        for _ in range(nv):
+            if fill_v:
+                fill_v.pop(0)()
+
+    def decode(parts, k, c0):
+        big = float(OWN + PAD)
+        for C, key, sl in parts:
+            cp(T.Ci[:, sl], C, [key], ["Ci%d" % sl.start])
+        for C, key, sl in parts:
+            ts(T.tU[:, sl], C, float(2 ** 23), big, A.is_lt, MUL, [key], ["tU%d" % sl.start])
+        ts(T.ai[:, 0:k], T.Ci[:, 0:k], M_ - 1, None, AND, None, ["Ci0", "Ci1"], ["ai"])
+        ts(T.bi[:, 0:k], T.Ci[:, 0:k], 11, FAR * M_ - 1, SHR, AND, ["Ci0", "Ci1"], ["bi"])
+        tt(T.zU[:, 0:k], T.ai[:, 0:k], T.tU[:, 0:k], ADD, ["ai", "tU0", "tU1"], ["zU"])
+        ts(T.b4[:, 0:k], T.bi[:, 0:k], float(PAD), None, ADD, None, ["bi"], ["b4"])
+        ts(T.tX[:, 0:k], T.tU[:, 0:k], -1.0, big, MUL, ADD, ["tU0", "tU1"], ["tX"])
+        tt(T.Uf[:, 0:k], T.zU[:, 0:k], T.b4[:, 0:k], A.max, ["zU", "b4"], ["Uf"])
+        tt(T.zX[:, 0:k], T.ai[:, 0:k], T.tX[:, 0:k], ADD, ["ai", "tX"], ["zX"])
+        ts(T.UO[:, c0:c0 + k], T.Uf[:, 0:k], -float(PAD), None, ADD, None, ["Uf"], ["U%d" % c0])
+        tt(T.Xf[:, 0:k], T.zX[:, 0:k], T.b4[:, 0:k], A.max, ["zX", "b4"], ["Xf"])
+        ts(T.XO[:, c0:c0 + k], T.Xf[:, 0:k], -float(PAD), None, ADD, None, ["Xf"], ["X%d" % c0])
+
+    def clamp(lo, hi):
+        ts(T.Mc[:, lo:hi], T.Mb[:, lo:hi], 0.0, chi, A.max, A.min, ["Mb%d" % lo, "chi"], ["Mc%d" % lo])
+
+    f = OPT["f"]
+    VW = ((T.pv, "p:v"), (T.pw, "p:w"))
+    act(T.GU[:, 0:256], T.IU[:].indirect(T.AB[:, 0:16]), AF.Copy, IUA + ["A0"], ["GU"])
+    fill(f[0], f[1])
+    tt(T.Mb[:, 0:256], T.IU[:].indirect(T.AB[:, 16:32]), T.GU[:, 0:256], ADD, IUA + ["B0", "GU"], ["Mb0"])
+    clamp(0, 256)
+    mm([(T.pv[:, 0:16], sel(T.WL, s), T.Mc[:, s:256:16]) for s in range(16)], ["WL", "Mc0"], ["p:v"])
+    fill(f[2], f[3])
+    decode([(T.pv[:, 0:16], "p:v", slice(0, 16))], 16, 0)
+
+    def expand(k, c0, pa, pv_, na, nv):
+        n = 16 * k
+        act(T.GU[:, 0:n], T.IU[:].indirect(T.UO[:, c0:c0 + k]), AF.Copy, IUA + ["U%d" % c0], ["GU"])
+        fill(pa + na, pv_)
+        tt(T.Mb[:, 0:n], T.IX[:].indirect(T.XO[:, c0:c0 + k]), T.GU[:, 0:n], ADD, IXA + ["X%d" % c0, "GU"], ["Mb0"])
+        clamp(0, n)
+        for h, (P_, key) in enumerate(VW):
+            mm([(P_[:, 0:k], sel(T.WE, 2 * s), T.Mc[:, 8 * h + s:n:16]) for s in range(8)], ["WE", "Mc0"], [key])
+        fill(0, nv)
+        decode([(T.pv[:, 0:k], "p:v", slice(0, 2 * k, 2)), (T.pw[:, 0:k], "p:w", slice(1, 2 * k, 2))], 2 * k, c0 + k)
+
+    expand(16, 0, f[4], f[5], f[6], f[7])
+    expand(32, 16, 0, f[8], f[9], f[10])
+    fill(20, 20)
+
+    act(T.nU[:, 1024:1792], T.H[:].indirect(T.UO[:, 0:48]), AF.Identity, HA + ["U0", "U16"], ["nUe"], scale=-1.0)
+    tt(T.VL[:, 1024:1792], T.HL[:].indirect(T.XO[:, 0:48]), T.nU[:, 1024:1792], A.is_lt, HLA + ["X0", "X16", "nUe"], ["VLe"])
+    tt(T.VR[:, 1024:1792], T.HR[:].indirect(T.XO[:, 0:48]), T.nU[:, 1024:1792], A.is_lt, HRA + ["X0", "X16", "nUe"], ["VRe"])
+    for h in range(2):
+        mm([(T.pm[:, h, 0:48], sel(T.BK, 2 * s + e), Vb[:, 1024 + 8 * h + s:1792:16]) for e, Vb in ((0, T.VL), (1, T.VR)) for s in range(8)],
+           ["BK", "VLe", "VRe"], ["p:m%d" % h])
+
+    def early_d2():
+        for h in range(2):
+            cp(T.d2[:, h:32:2], T.pm[:, h, 0:16], ["p:m%d" % h], ["d2%d" % h])
+        for h, (P_, key) in enumerate(VW):
+            mm([(P_[:, 0:32], T["PM%d" % h][:], T.d2[:])], ["PM%d" % h, "d20", "d21"], [key])
+            cp(T.d3[:, 32 * h:32 * h + 32], T.pm[:, h, 16:48], ["p:m%d" % h], ["d3%d" % h])
+
+    def early_dead():
+        for h, (P_, key) in enumerate(VW):
+            tt(T.dead[:, h:64:2], P_[:, 0:32], T.d3[:, 32 * h:32 * h + 32], ADD, [key, "d3%d" % h], ["dead%d" % h])
+
+    cuts, mc = OPT["cuts"], OPT["mc"]
+    nc = len(cuts) - 1
+    VLK, NU, DK = ["VL%d" % i for i in range(nc)], ["nU%d" % i for i in range(nc)], ["dead0", "dead1"]
+
+    def mask_l(i):
+        mm([(T.pm[:, i, :], T.ML[:], T.VL[:, 512 * i:512 * i + 512])], ["ML"] + VLK, ["p:m%d" % i], stop=False)
+
+    def mask_r(i):
+        mm([(T.pm[:, i, :], T.MR[:], T.VR[:, 512 * i:512 * i + 512])], ["MR", "VR", "VR0"], ["p:m%d" % i], start=False)
+        act(T.mk[:, 512 * i:512 * i + 512], T.pm[:, i, :], AF.Sigmoid, ["p:m%d" % i, "cbm"], ["mk%d" % i], bias=cbm, scale=256.0)
+
+    for r in range(4):
+        last = r == 3
+        c0 = 48 + 64 * r
+        xk, uk = "X%d" % c0, "U%d" % c0
+        wn, wk = wins[r], "win%d" % r
+
+        def test(Vb, tab, a_, b_, R, W):
+            tt(Vb[:, 16 * a_:16 * b_], tab[:].indirect(T.XO[:, c0 + a_:c0 + b_]), T.nU[:, 16 * a_:16 * b_], A.is_lt, R + [xk], W)
+
+        def mpart(lo, hi):
+            tt(T.Mb[:, lo:hi], T.IX[:].indirect(T.XO[:, c0 + lo // 16:c0 + hi // 16]), T.GU[:, lo:hi], ADD, IXA + [xk, "GU"], ["Mb%d" % lo])
+
+        for i in range(nc):
+            a_, b_ = cuts[i], cuts[i + 1]
+            act(T.nU[:, 16 * a_:16 * b_], T.H[:].indirect(T.UO[:, c0 + a_:c0 + b_]), AF.Identity, HA + [uk], ["nU%d" % i], scale=-1.0)
+        act(T.GU[:], T.IU[:].indirect(T.UO[:, c0:c0 + 64]), AF.Copy, IUA + [uk], ["GU"])
+        for i in range(nc):
+            test(T.VL, T.HL, cuts[i], cuts[i + 1], HLA + ["nU%d" % i], ["VL%d" % i])
+            if i == 0:
+                test(T.VR, T.HR, 0, cuts[1], HRA + ["nU0"], ["VR0"])
+            if r == 0 and i == nc - 2:
+                early_d2()
+            if r == 0 and i == nc - 1:
+                early_dead()
+        mm([(T.pc[:, 0, 0:64], T.Idn[:], T.dead[:])] + [(T.pc[:, 0, 0:64], sel(T.BK, s), T.VL[:, s:1024:16]) for s in range(16)],
+           ["Idn", "BK"] + DK + VLK, ["p:c0"])
+        mask_l(0)
+        test(T.VR, T.HR, cuts[1], 64, HRA + NU, ["VR"])
+        mm([(T.pc[:, 1, 0:64], T.Idn[:], T.dead[:])] + [(T.pc[:, 1, 0:64], sel(T.BK, s), T.VR[:, s:1024:16]) for s in range(16)],
+           ["Idn", "BK", "VR", "VR0"] + DK, ["p:c1"])
+        mask_r(0)
+        tt(T.T1[:], T.pc[:, 0, 0:64], T.JD[:], A.min, ["p:c0", "JD"], ["T1"])
+        mpart(0, mc)
+        ts(T.kk[:], T.pc[:, :, 0:64], 0.0, None, EQ, None, ["p:c0", "p:c1"], ["kk"])
+        mm([(T.pt[:, 0:64], T.Blk[:], T.kk[:, e, :]) for e in range(2)], ["Blk", "kk"], ["p:t"])
+        mm([(T.pb[:, 0:64], T.Tri[:], T.kk[:, e, :]) for e in range(2)], ["Tri", "kk"], ["p:b"])
+        mask_l(1)
+        mask_r(1)
+        tt(T.T2[:], T.pc[:, 1, 0:64], T.T1[:], A.min, ["p:c1", "T1"], ["T2"])
+        mpart(mc, 1024)
+        op("v", lambda: V.tensor_tensor_scan(T.S[:, 1:65], T.pt[:, 0:64], T.Z0[:], 0.0, ADD, ADD), ["p:t", "Z0"], ["S"])
+        tt(T.O2[:], T.pb[:, 0:64], T.T2[:], ADD, ["p:b", "T2"], ["O2"])
+        if not last:
+            clamp(0, mc)
+        tt(T.O[:], T.S[:, 0:64], T.O2[:], ADD, ["S", "S0", "O2"], ["O"])
+        if not last:
+            clamp(mc, 1024)
+        ts(T.off[:], T.O[:], 1.0, None, ADD, None, ["O"], ["off"])
+        src, sk = (T.Mb, "Mb") if last else (T.Mc, "Mc")
+        tt(wn[:].indirect(T.off[:]), src[:], T.mk[:], MUL, ["off", sk + "0", sk + str(mc), "mk0", "mk1"], [wk])
+        cur, prv, both = ("WC0", "WP0", "WN0") if last else ("WC", "WP", "WN")
+        P_, key = VW[last]
+        mm([(P_[:, 0:64], sel(T[both if s < 15 else cur], s), wn[:, 1 + s:1010 + s:16]) for s in range(16)]
+           + [(P_[:, 0:64], sel(T[prv], 0), wn[:, 0:1009:16])], [cur, prv, both, wk], [key])
+        if not last:
+            ts(T.dead[:], T.JC[:], T.S[:, 64:65], 4096.0, A.is_ge, MUL, ["JC", "S"], DK)
+            decode([(T.pv[:, 0:64], "p:v", slice(0, 64))], 64, c0 + 64)
+
+    mm([(T.pv[:, 0:64], sel(T[x], s), wn[:, o + 64 * s:o + 64 * s + 64]) for s in range(16) for x, o in ((cur, 1), (prv, 0))],
+       [cur, prv, wk], ["p:v"])
+    ts(T.df[:], T.J0[:], T.S[:, 64:65], None, A.is_ge, None, ["J0", "S"], ["df"])
+    ts(T.al[:], T.J0[:], T.S[:, 64:65], None, A.is_lt, None, ["J0", "S"], ["al"])
+
+    def split(C, key):
+        cp(T.Ci[:], C, [key], ["Ci0"])
+        ts(T.ai[:], T.Ci[:], M_ - 1, None, AND, None, ["Ci0"], ["ai"])
+        ts(T.bi[:], T.Ci[:], 11, None, SHR, None, ["Ci0"], ["bi"])
+
+    split(T.pw[:, 0:64], "p:w")
+    ts(T.FA[:, 0:64], T.ai[:], float(OWN), None, ADD, None, ["ai"], ["FA"])
+    cp(T.FA[:, 64:128], T.bi[:], ["bi"], ["FB"])
+    fc = OPT["fc"]
+    for i in range(len(fc) - 1):
+        a_, b_ = fc[i], fc[i + 1]
+        act(T.VL[:, 64 * a_:64 * b_], T.H[:].indirect(T.FA[:, 4 * a_:4 * b_]), AF.Copy, HA + ["FA"], VLK if i == 0 else ["fl%d" % i])
+        cp(T.VR[:, 64 * a_:64 * b_], T.H[:].indirect(T.FA[:, 64 + 4 * a_:64 + 4 * b_]), HA + ["FB"], ["VR", "VR0"] if i == 0 else ["fr%d" % i])
+        mm([(T.pc[:, 0, 0:64], sel(T.B1, s), Vb[:, 64 * s:64 * s + 64]) for Vb in (T.VL, T.VR) for s in range(a_, b_)],
+           ["B1", "VL0", "VR", "fl%d" % i, "fr%d" % i], ["p:c0"], start=i == 0, stop=i == len(fc) - 2)
+    split(T.pv[:, 0:64], "p:v")
+    tt(T.oa[:], T.ai[:], T.df[:], A.subtract, ["ai", "df"], ["oa"])
+    tt(T.ob[:], T.bi[:], T.df[:], A.subtract, ["bi", "df"], ["ob"])
+    dma("s", T.ya[:], T.oa[:], "outs", ["oa"], [])
+    dma("a", T.yb[:], T.ob[:], "outs", ["ob"], [])
+    tt(T.oz[:], T.pc[:, 0, 0:64], T.al[:], MUL, ["p:c0", "al"], ["oz"])
+    dma("s", T.ys[:], T.oz[:], "outs", ["oz"], [])
+    for s in sorted(total, key=lambda s: s == "outs"):
+        if max(seen[q].get(s, 0) for q in Q) < total[s]:
+            g.wait_ge(T.sem[s], total[s])

@@ -2,33 +2,36 @@ from concourse.bass import DstId, RemoteDMATransfer
 from concourse.mybir import AluOpType as A, ActivationFunctionType as AF
 
 M_, FAR, F_ = 2048, 2, 1024
-PAD, OWN, TW = 4096, 4112, 6160
-WW = 5128
-KX = 112 + 64 * 3
-OPT = {"hra": 1, "f": [2, 0, 2, 2, 4, 6, 3, 2, 1, 3, 2], "cuts": [0, 8, 24, 44, 64], "mc": 640, "fc": [0, 7, 13, 16]}
+XW, GAP, OWNU, UW = 6144, 4096, 6144, 8192
+DUMP, WW, WZ = 4100, 9344, 2064
+BIG, MM = float(2 ** 22), float(2 ** 23)
+KX = 48 + 64 * 4
+OPT = {"cuts": [0, 12, 32, 64], "fc": [("a", 0, 10), ("v", 18, 32), ("a", 10, 18)], "c1": 2,
+       "f": [4, 7, 1, 2, 6, 0, 0, 0, 0, 0, 0, 99], "to": "vava", "lin": 24, "kp": "aaav",
+       "early": [[], [], [(1, 0, 1)], [(1, 1, 3)], [(0, 0, 3)]], "gp": 0, "gq": 4, "gap": 1008, "lf": [("a", 0, 4), ("v", 4, 8)]}
 
 SCRATCH = {}
 for _n, _c, _d in (
-        ("hs", [M_], "bfloat16"), ("HL HR", [TW], "bfloat16"), ("H", [TW + 16], "bfloat16"), ("IX", [TW], "float32"),
-        ("IU UR", [TW + 16], "float32"), ("G", [4096], "float32"),
-        ("GU", [1024], "float32"), ("nU VL VR", [1792], "bfloat16"), ("Mb Mc mk", [1024], "bfloat16"),
-        ("win0 win1 win2 win3", [WW], "bfloat16"), ("KL KR vI Wi", [128], "int32"), ("SA SB", [16], "int32"),
-        ("kin ti tj tf tg Po Pf", [256], "float32"), ("lin lsend", [512], "uint16"), ("lown", [256], "uint16"),
-        ("ksend kown ui uh vf uf ug lf lb ls r0", [128], "float32"), ("XO UO", [KX], "uint16"), ("AB", [32], "uint16"),
-        ("off", [64], "uint16"), ("FA", [128], "uint16"), ("pI ci cj", [4], "int32"), ("xI", [256], "int32"),
-        ("jI Ci ai bi", [64], "int32"), ("cf cq oe oer ov c256 w1 w0", [4], "float32"), ("cc", [16], "float32"),
-        ("CB", [24], "float32"), ("B1 B2 B3 BK WL WE WP WC WN WP0 WC0 WN0", [144], "bfloat16"),
-        ("Blk ML MR Tri Idn PM0 PM1", [128], "bfloat16"),
-        ("J0 JC JD Z0 O2 d3 tU tX zU zX b4 Xf Uf T1 T2 O df al oa ob oz", [64], "float32"), ("P2", [8, 16], "float32"),
-        ("TI TO", [8, 32], "float32"), ("LR", [2, 128], "int32"), ("kk", [2, 64], "bfloat16"),
-        ("S", [72], "float32"), ("dead", [64], "bfloat16"), ("d2", [32], "bfloat16")):
+        ("K", [M_ + 16], "bfloat16"), ("H", [UW + 16], "bfloat16"), ("HL HR TX", [XW], "bfloat16"), ("hs gL gR Tf Lf", [M_], "bfloat16"),
+        ("nU VL VR St", [1792], "bfloat16"), ("Tg Mc", [1024], "bfloat16"), ("P0 P1 XB LF", [256], "bfloat16"),
+        ("P2 Qb Mb", [512], "bfloat16"), ("Qi Qm", [512], "int32"),
+        ("win0 win1 win2 win3", [WW], "bfloat16"), ("KL KR Wi Li Ri", [128], "int32"), ("SA SB Cs", [16], "int32"), ("Di", [64], "int32"),
+        ("xF", [160], "float32"), ("X8 vf ls r0", [128], "float32"), ("dd", [136], "float32"), ("lf", [128], "bfloat16"), ("MX", [276, 8], "bfloat16"),
+        ("TI", [8, 32], "float32"),
+        ("TO", [256], "float32"), ("lown", [384], "uint16"), ("lin", [512], "uint16"), ("XO UO", [KX], "uint16"), ("AB off", [64], "uint16"), ("D3", [48], "uint16"),
+        ("lo8", [8], "uint16"), ("FA", [128], "uint16"), ("ci", [8], "int32"), ("cf O8 KB", [8], "float32"), ("cc", [64], "float32"),
+        ("O4 Or", [4], "float32"), ("O16 ta tb tc", [16], "float32"), ("Ci ai bi", [64], "int32"),
+        ("BK WC WR WN Zs", [144], "bfloat16"), ("Cm Idn Blk2 Tri2 TriL Rst2 RstL WM ga gb", [128], "bfloat16"),
+        ("J0 JC JD mn mx T1 df dg al oa ob oz", [64], "float32"), ("kk", [2, 66], "bfloat16"),
+        ("S T2 dT", [72], "float32"), ("dead", [64], "bfloat16")):
     for _x in _n.split():
         SCRATCH[_x] = ("sbuf", [128] + _c, _d)
-SCRATCH.update({"pc": ("psum", [128, 2, 512], "float32"), "pm": ("psum", [128, 2, 512], "float32"),
-                "pv": ("psum", [128, 512], "float32"), "pw": ("psum", [128, 512], "float32"),
-                "pb": ("psum", [128, 512], "float32"), "pt": ("psum", [128, 512], "float32")})
-SEMAPHORES = ["sv", "sa_", "sp", "sg", "lhs", "lkl", "lkr", "lsa", "lsb", "lsw", "kown", "kowr", "kfu", "kfr", "outs",
-              "sent", "arrh", "arri", "farh", "fari"]
+for _x in ("pA", "pB", "pC", "pD"):
+    SCRATCH[_x] = ("psum", [128, 2, 512], "float32")
+SEMAPHORES = ["sv", "sa_", "sp", "sg", "lhs", "lkl", "lkr", "lsa", "lsb", "lsw", "lhl", "outs", "sent",
+              "arr0", "arr1", "arr2", "arr3", "far0", "far1", "far2", "far3"]
+MSGS = ((0, 4), (1, 8), (2, 8), (3, 4))
+MXO = {"Y": 0, "G": 64, "Ihi": 128, "Ilo": 146, "W3o": 164, "W3f": 180, "WT": 196, "WU": 212, "WS": 228, "WCL": 244, "WCR": 260}
 
 
 def helpers_of(T, topo, q):
@@ -38,7 +41,7 @@ def helpers_of(T, topo, q):
     ok = [c for c in topo.cores_of(src) if c != src and all(topo.may_write(c, x) for x in dsts)]
     near = [c for c in ok if topo.die(c) == topo.die(src)]
     other = [c for c in ok if topo.die(c) != topo.die(src)]
-    return near[:2] + other[:2], dsts
+    return [near[0], other[0], near[1], other[1]], dsts
 
 
 def bits(engs):
@@ -53,8 +56,8 @@ def dst_id(topo, dst, src):
     return DstId(rid=rid, pnc=pid)
 
 
-def info_helper(hs_, d):
-    return hs_[(2 * d) % len(hs_)]
+def stage(T, m):
+    return T.lown[:, 0:256] if m == 1 else T.gL[:, 512 * m:512 * m + 512]
 
 
 def helper_program(g, core, T, topo):
@@ -65,26 +68,19 @@ def helper_program(g, core, T, topo):
         i = hs_.index(core)
         w = M_ // len(hs_)
         sent = 0
-        for d, x in enumerate(dsts):
-            if topo.may_write(T.cores[q], x) or info_helper(hs_, d) != core:
+        for m, n in MSGS:
+            if m == 1 and i != 0:
                 continue
-            g.wait_ge(T.sem.arri, 8)
-            e = topo.engines(core, x)
-            ks, ls = T.kin[:, 128 * d:128 * d + 128], T.lin[:, 256 * d:256 * d + 256]
-            g.remote_dma_fused([
-                RemoteDMATransfer(dst_ids=[dst_id(topo, x, core)], dma_engine_mask=bits(e[0:4]), remote_sem=T.sem.fari, src=ks, dst=ks),
-                RemoteDMATransfer(dst_ids=[dst_id(topo, x, core)], dma_engine_mask=bits(e[4:8]), remote_sem=T.sem.fari, src=ls, dst=ls),
-            ], local_sem=T.sem.sent)
-            sent += 8
-        g.wait_ge(T.sem.arrh, 4)
-        tr = []
-        for d, x in enumerate(dsts):
-            e = topo.engines(core, x)
-            c0 = d * M_ + i * w
-            tr.append(RemoteDMATransfer(dst_ids=[dst_id(topo, x, core)], dma_engine_mask=bits(e[4 * d:4 * d + 4]),
-                                        remote_sem=T.sem.farh, src=T.HL[:, 0:w], dst=T.H[:, c0:c0 + w]))
-        g.remote_dma_fused(tr, local_sem=T.sem.sent)
-        sent += 4 * len(dsts)
+            g.wait_ge(T.sem["arr%d" % m], n)
+            tr = []
+            for d, x in enumerate(dsts):
+                c0 = d * M_ + i * w
+                dst = (T.H[:, c0:c0 + w], T.lin[:, 128 * d:128 * d + 128], T.TX[:, M_ + c0:M_ + c0 + w], T.HL[:, M_ + c0:M_ + c0 + w])[m]
+                src = T.lown[:, 128 * d:128 * d + 128] if m == 1 else stage(T, m)
+                tr.append(RemoteDMATransfer(dst_ids=[dst_id(topo, x, core)], dma_engine_mask=bits(topo.engines(core, x)[4 * d:4 * d + 4]),
+                                            remote_sem=T.sem["far%d" % m], src=src, dst=dst))
+            g.remote_dma_fused(tr, local_sem=T.sem.sent)
+            sent += 4 * len(dsts)
         g.wait_ge(T.sem.sent, sent)
 
 
@@ -97,6 +93,7 @@ def rank_program(g, core, T, topo):
     esem = {"v": "sv", "a": "sa_", "p": "sp", "g": "sg"}
     total = {}
     seen = {k: {} for k in Q}
+    alone = [False]
     wr, rd = {}, {}
 
     def wait(q, tok):
@@ -132,6 +129,10 @@ def rank_program(g, core, T, topo):
     def op(q, fn, R, W):
         before(q, R, W)
         s = esem[q]
+        if q == "g" and s in total and (alone[0] or "XB" in R):
+            wait(q, (s, None))
+        if q == "g":
+            alone[0] = "XB" in R
         fn().then_inc(T.sem[s], 1)
         total[s] = total.get(s, 0) + 1
         after((s, total[s]), R, W)
@@ -167,399 +168,513 @@ def rank_program(g, core, T, topo):
     def ms(out, c, W):
         op("v", lambda: V.memset(out, c), [], W)
 
-    def act(out, in_, f, R, W, **kw):
+    def act(out, in_, R, W, f=AF.Identity, **kw):
         op("a", lambda: g.scalar.activation(out, in_, f, **kw), R, W)
 
-    def fiota(name, pat, base):
-        op("g", lambda: g.iota(T[name][:], pat, base, 0, allow_small_or_imprecise_dtypes=True), [], [name])
+    def fiota(out, pat, W, R=(), base=0, cm=0):
+        op("g", lambda: g.iota(out, pat, base, cm, allow_small_or_imprecise_dtypes=True), R, W)
+
+    def asel(out, in_, pat, cmp_, fill_, base, cm, R, W):
+        op("g", lambda: g.affine_select(out, in_, pat, cmp_, fill_, base, cm), R, W)
 
     def sel(W_, s):
         return W_[:, 15 - s:143 - s]
 
-    AND, SHR, EQ, MUL, ADD = A.bitwise_and, A.logical_shift_right, A.is_equal, A.mult, A.add
+    def xs(lo, n, step=1):
+        return T.xF[:, 16 + lo:16 + lo + n * step:step]
+
+    AND, SHR, SAR, EQ, MUL, ADD = A.bitwise_and, A.logical_shift_right, A.arith_shift_right, A.is_equal, A.mult, A.add
     hs_, dsts = helpers_of(T, topo, rank)
+    nh = len(hs_)
+    total["sent"] = 0
+
+    def push(m, parts, R):
+        ne = dict(MSGS)[m]
+        before("g", R, [])
+        g.remote_dma_fused([RemoteDMATransfer(dst_ids=[dst_id(topo, hs_[i], core)],
+                                              dma_engine_mask=bits(topo.engines(core, hs_[i])[j % 2::2][ne * (j // 2):ne * (j // 2) + ne]),
+                                              remote_sem=T.sem["arr%d" % m], src=src, dst=stage(T, m))
+                            for j, (i, src) in enumerate(parts)], local_sem=T.sem.sent)
+        total["sent"] += ne * len(parts)
+
+    for m, key in enumerate(("Hf", "lin", "TXf", "HLf")):
+        total["far%d" % m] = 4 * FAR * (1 if m == 1 else nh)
+        wr[key] = ("far%d" % m, None)
+
+    C = {}
+
+    def lin(name, x, a, b=0.0):
+        n = len([1 for z in C.values() if z[1].startswith("c_")])
+        col = T.cc[:, n:n + 1]
+        (xc, xk), R = C[x], []
+        if isinstance(a, str):
+            R.append(C[a][1])
+            a = C[a][0]
+        if isinstance(b, str):
+            R.append(C[b][1])
+            b = C[b][0]
+        act(col, xc, [xk] + R, ["c_" + name], scale=a, bias=b)
+        C[name] = (col, "c_" + name)
+
+    def eqm(out, pat, pk, tgt, val, W):
+        if val is None:
+            ts(out, pat, C[tgt][0], None, EQ, None, [pk, C[tgt][1]], W)
+        elif isinstance(val, str):
+            ts(out, pat, C[tgt][0], C[val][0], EQ, MUL, [pk, C[tgt][1], C[val][1]], W)
+        else:
+            ts(out, pat, C[tgt][0], val, EQ, MUL, [pk, C[tgt][1]], W)
+
+    def mx(name, lo=0):
+        return T.MX[:, MXO[name] + lo:MXO[name] + lo + 16, :]
+
+    def dist(d, pat, pk, tgt):
+        act(d, pat, [pk, C[tgt][1]], ["dist"], f=AF.Abs, scale=-1.0, bias=C[tgt][0])
+
+    def eqa(out, d, val, W):
+        act(out, d, ["dist", C[val][1]], W, f=AF.Relu, scale=-1.0, bias=C[val][0])
 
     dma("s", T.KL[:], T.kl[:], "lkl", [], ["KL"])
-    dma("a", T.KR[:], T.kr[:], "lkr", [], ["KR"])
-    dma("s", T.hs[:], T.h[:], "lhs", [], ["hs"])
-    dma("s", T.H[0::2, OWN:TW], T.h[1::2, :], "lsw", [], ["Ho0"])
-    dma("s", T.H[1::2, OWN:TW], T.h[0::2, :], "lsw", [], ["Ho1"])
+    dma("a", T.hs[:, 0:M_], T.h[:], "lhs", [], ["hs"])
+    dma("s", T.KR[:], T.kr[:], "lkr", [], ["KR"])
     dma("s", T.SA[:], T.sa[:], "lsa", [], ["SA"])
     dma("s", T.SB[:], T.sb[:], "lsb", [], ["SB"])
+    dma("s", T.H[0::2, OWNU:UW], T.h[1::2, :], "lsw", [], ["Ho0"])
+    dma("s", T.H[1::2, OWNU:UW], T.h[0::2, :], "lsw", [], ["Ho1"])
 
-    op("g", lambda: g.iota(T.pI[:, 0:1], [[0, 1]], 0, 1), [], ["pI"])
-    op("g", lambda: g.iota(T.xI[:], [[1, 256]], 0, 0), [], ["xI"])
-    op("g", lambda: g.iota(T.vI[:], [[1, 128]], 0, 128), [], ["vI"])
-    fiota("ti", [[0, 8], [8, 32]], 0)
-    fiota("tj", [[1, 8], [0, 32]], 0)
-    op("g", lambda: g.iota(T.jI[:], [[1, 64]], 0, 64), [], ["jI"])
-    fiota("ui", [[1, 8], [0, 16]], 0)
-    fiota("uf", [[0, 16], [2, 2], [0, 4]], -1)
-    fiota("ug", [[0, 8], [-17, 4], [0, 4]], 0)
-    fiota("uh", [[1, 64], [0, 2]], 0)
-    fiota("JC", [[16, 64]], 0)
-    p = T.pI[:, 0:1]
-    ms(T.c256[:], 256.0, ["c256"])
-    ms(T.H[:, PAD:OWN], -262144.0, ["Hp"])
-    ts(T.ci[:, 0:1], p, 3, None, AND, None, ["pI"], ["ci0"])
-    ts(T.ci[:, 1:2], p, 2, 3, SHR, AND, ["pI"], ["ci1"])
-    ts(T.ci[:, 2:3], p, 4, None, SHR, None, ["pI"], ["ci2"])
-    ts(T.ci[:, 3:4], p, 4, 1, SHR, AND, ["pI"], ["ci3"])
-    ms(T.S[:, 0:1], 0.0, ["S0"])
-    cp(T.cf[:], T.ci[:], ["ci0", "ci1", "ci2", "ci3"], ["cf"])
-    for name in ("IU", "UR", "HL", "HR", "IX"):
-        ms(T[name][:, PAD:OWN], 0.0, [name + "p"])
-    ce, cv, cg, ch = (T.cf[:, i:i + 1] for i in range(4))
-    c15, cmR, chi, csg, ch0, cpf, cbm, c2, c3, cnz, cpm = (T.cc[:, i:i + 1] for i in range(11))
-    act(csg, cv, AF.Sigmoid, ["cf"], ["csg"], bias=384.0, scale=-256.0)
-    ts(T.oe[:], T.xI[:, 0:4], ce, None, EQ, None, ["xI", "cf"], ["oe"])
-    ts(T.ov[:], T.xI[:, 0:4], cv, None, EQ, None, ["xI", "cf"], ["ov"])
-    e0, e1, e2, e3 = (T.oe[:, i:i + 1] for i in range(4))
-    v0, v1, v2, v3 = (T.ov[:, i:i + 1] for i in range(4))
-    ts(T.Po[:], T.xI[:], e0, None, MUL, None, ["xI", "oe"], ["Po"])
-    ts(T.CB[:, 16:24], T.xI[:, 0:8], e1, None, MUL, None, ["xI", "oe"], ["CBo"])
-    ts(c15, cg, 16.0, 15.0, MUL, ADD, ["cf"], ["c15"])
-    ts(ch0, ch, -1.0, 1.0, MUL, ADD, ["cf"], ["ch0"])
-    ts(cmR, v0, -1.0, 1.0, MUL, ADD, ["ov"], ["cmR"])
-    ts(T.B1[:], T.xI[:, 0:144], c15, None, EQ, None, ["xI", "c15"], ["B1"])
-    ts(T.vI[:], T.vI[:], M_ - 1, None, AND, None, ["vI"], ["vI"])
-    ts(T.CB[:, 0:16], T.xI[:, 0:16], 8.0, e2, MUL, MUL, ["xI", "oe"], ["CBf"])
-    ts(T.vf[:], T.vI[:], float(2 ** 22), None, ADD, None, ["vI"], ["vf"])
-    ms(T.H[:, TW:TW + 16], -262144.0, ["Hq"])
-    ms(T.IU[:, TW:TW + 16], 0.0, ["IUq"])
-    ms(T.UR[:, TW:TW + 16], 0.0, ["URq"])
-    ts(T.tf[:], T.ti[:], e1, None, MUL, None, ["ti", "oe"], ["tf"])
+    op("g", lambda: g.iota(T.ci[:, 0:1], [[0, 1]], 0, 1), [], ["p"])
+    fiota(T.xF[:], [[1, 160]], ["xF"], base=-16)
+    fiota(T.X8[:], [[16, 8], [0, 2], [1, 8]], ["X8"])
+    fiota(T.XB[:], [[1, 256]], ["XB"])
+    fiota(T.XB[64:65, :], [[1, 8], [0, 32]], ["XB2"], ["XB"])
+    p = T.ci[:, 0:1]
+    ms(T.Zs[:, 0:3], 0.0, ["Zs0"])
+    ms(T.Cm[0:65, :], 0.0, ["Cm"])
+    for j, m_ in ((1, 15), (2, 7), (3, 16), (4, 8), (5, 112), (7, 3)):
+        ts(T.ci[:, j:j + 1], p, m_, None, AND, None, ["p"], ["ci%d" % j])
+    ts(T.ci[:, 6:7], p, 2, 3, SHR, AND, ["p"], ["ci6"])
+    ms(T.MX[:, MXO["Ilo"], :], 0.0, ["Ilo0"])
+    cp(T.cf[:], T.ci[:], ["p"] + ["ci%d" % j for j in range(1, 8)], ["cf"])
+    for j, name in enumerate(("p", "k", "k8", "p16", "hi8", "g16", "r4", "i4")):
+        C[name] = (T.cf[:, j:j + 1], "cf")
+    ms(T.MX[:, MXO["WU"]:MXO["WS"] + 16, :], 0.0, ["WU", "WS"])
+    lin("tY", "r4", 1.0, "g16")
+    lin("lo0", "k8", 32.0, "p16")
+    lin("vb", "k", 128.0, MM)
+    lin("lo1", "hi8", 0.125, "lo0")
+    eqm(T.O4[:], xs(0, 4), "xF", "i4", None, ["O4"])
+    eqm(T.Or[:], xs(0, 4), "xF", "r4", None, ["Or"])
+    eqm(T.O16[:], xs(0, 16), "xF", "k", None, ["O16"])
+    eqm(T.O8[:], xs(0, 8), "xF", "k8", None, ["O8"])
+    for j in range(4):
+        C["i%d" % j] = (T.O4[:, j:j + 1], "O4")
+        C["r%d" % j] = (T.Or[:, j:j + 1], "Or")
+    for j in range(16):
+        C["e%d" % j] = (T.O16[:, j:j + 1], "O16")
+    for j in range(8):
+        C["o%d" % j] = (T.O8[:, j:j + 1], "O8")
+    ts(T.vf[:], xs(0, 128), C["vb"][0], None, ADD, None, ["xF", "c_vb"], ["vf"])
+    ts(T.Zs[:, 3:131], T.X8[:], 4.0, C["g16"][0], A.subtract, EQ, ["X8", "cf"], ["Zs"])
+    ts(T.lo8[:], xs(0, 8), 2.0, C["lo1"][0], MUL, ADD, ["xF", "c_lo1"], ["lo8"])
+    eqm(T.Zs[:, 11:131:16], xs(0, 8, 16), "xF", "g16", None, ["Zs"])
+    d_ = T.dd[:, 0:128]
+    dist(d_, xs(0, 128), "xF", "tY")
+    lin("tG", "tY", 1.0, 3.0)
+    for j in range(4):
+        eqa(mx("Y", 16 * j), d_, "i%d" % j, ["Y%d" % j])
+    for c in (("qs0", "r2", 1.0 / 256 - 1, 1.0), ("qo0", "r2", -0.5 + 1.0 / 512), ("qt0", "r0", BIG - 1, 1.0), ("qu", "r3", -float(2 ** 20)),
+              ("qs", "r3", 1.0 / 65536 - 1, "qs0"), ("qo", "r3", 16 - 0.5 + 1.0 / 131072, "qo0")):
+        lin(*c)
+    dist(d_, T.X8[:], "X8", "tG")
+    for c in (("qt1", "r2", 255.0, "qt0"), ("kb", "e10", 8.0, "e1"), ("hi", "hi8", 0.125), ("t8", "hi8", -1.0, "p"), ("qt", "r3", 65535.0, "qt1")):
+        lin(*c)
+    for j in range(4):
+        eqa(mx("G", 16 * j), d_, "i%d" % j, ["G%d" % j])
+    lin("t3", "o3", 4.0, "t8")
+    lin("lo", "hi", -1.0, 1.0)
+    dist(T.dd[:], xs(0, 136), "xF", "p")
+    act(T.KB[:], xs(0, 8), ["xF", "c_kb"], ["KB"], scale=C["kb"][0])
+    eqa(T.MX[:, MXO["Ihi"]:MXO["Ihi"] + 17, :], T.dd[:], "hi", ["Ihi"])
+    eqa(mx("Ilo", 1), d_, "lo", ["Ilo"])
+    lin("bf0", "e7", -MM)
+    dist(d_, T.X8[:], "X8", "t3")
+    lin("bf", "e15", 1.0, "bf0")
+    eqa(mx("W3f"), d_, "r2", ["W3f"])
+    eqa(mx("W3o"), d_, "r0", ["W3o"])
+    cols = [("bo0", "e15", -MM), ("e45", "o4", 1.0, "o5"), ("w0", "o1", 256.0, "o0"), ("bo", "e7", 1.0, "bo0"), ("u0", "o3", -1.0, "o6"),
+            ("w1", "o2", 65536.0, "w0"), ("m4", "r0", 1.0, "r2"), ("u", "e45", 1.0, "u0"), ("w", "e45", -float(2 ** 24), "w1"),
+            ("y8", "k8", -1.0, "p"), ("sd", "e1", 1.0 / 8192), ("wL", "w", "lo"), ("chF", "e45", -BIG, BIG), ("c2", "hi", 1.0, "g16"),
+            ("wR", "w", "hi"), ("ch0", "o4", 1.0, "chF"), ("g32", "g16", 2.0), ("ch", "o5", 1.0, "ch0"), ("g2k", "g16", 128.0)]
+    for q_, j, x in ((0, 0, 1.0), (64, 10, 1.0), (0, 9, 8.0), (64, 9, -256.0)):
+        wr["Cm%d" % (q_ + j)] = wr["Cm"]
+        ms(T.Cm[q_:q_ + 1, j:128:16], x, ["Cm%d" % (q_ + j)])
+    ms(T.H[:, GAP:GAP + 16], -262144.0, ["Hp"])
+    ms(T.K[:, M_:M_ + 16], 0.0, ["Kp"])
+
+    push(0, [(i, T.hs[:, 512 * i:512 * i + 512]) for i in range(nh)], ["hs"])
+
     ts(T.lf[:], T.KL[:], 0.0, None, EQ, None, ["KL"], ["lf"])
     ts(T.r0[:], T.KR[:], 2048.0, None, MUL, None, ["KR"], ["r0"])
-    ts(T.tg[:], T.tj[:], e2, None, MUL, None, ["tj", "oe"], ["tg"])
     tt(T.ls[:], T.lf[:], T.vf[:], MUL, ["lf", "vf"], ["ls"])
-    tt(T.Pf[:], T.tf[:], T.tg[:], ADD, ["tf", "tg"], ["Pf"])
-
-    def blk(b):
-        return (256 * b, T.Pf, "Pf", "CBf") if b < 16 else (OWN + 256 * (b - 16), T.Po, "Po", "CBo")
-
-    def iu_blk(b):
-        c, P_, k1, k2 = blk(b)
-        act(T.IU[:, c:c + 256], P_[:], AF.Identity, [k1, k2], ["IU%d" % b], bias=T.CB[:, b:b + 1])
-
-    def ur_blk(b):
-        c, P_, k1, k2 = blk(b)
-        ts(T.UR[:, c:c + 256], P_[:], T.CB[:, b:b + 1], cmR, ADD, MUL, [k1, k2, "cmR"], ["UR%d" % b])
-
-    for b in list(range(16, 24)) + list(range(16)):
-        iu_blk(b)
-    IUF, IUO = ["IU%d" % b for b in range(16)], ["IU%d" % b for b in range(16, 24)]
-    URF, URO = ["UR%d" % b for b in range(16)], ["UR%d" % b for b in range(16, 24)]
-
+    mm([(T.pA[:, 0, :], T.Zs[:, 3 - i:131 - i], T.hs[:, 512 * i:512 * i + 512]) for i in range(4)], ["Zs0", "Zs", "hs"], ["p:A0"], stop=False)
+    mm([(T.pA[:, 0, 128 * j:128 * j + 128], mx("Y", 16 * j), T.lf[:]) for j in range(4)], ["lf", "Y0", "Y1", "Y2", "Y3"], ["p:A0"], start=False)
     tt(T.r0[:], T.r0[:], T.KL[:], ADD, ["r0", "KL"], ["r0"])
-    mm([(T.pv[:, 0:128], sel(T.B1, s), T.hs[:, 128 * s:128 * s + 128]) for s in range(16)], ["B1", "hs"], ["p:v"])
-    ts(T.lb[:], T.lf[:], float(2 ** 22), None, MUL, None, ["lf"], ["lb"])
-    tt(T.P2[:], T.r0[:], T.ls[:], ADD, ["r0", "ls"], ["P2a"])
-    ts(T.TI[:, :, 0:16], T.P2[:], ch0, None, MUL, None, ["P2a", "ch0"], ["TI0"])
-    ts(T.TI[:, :, 16:32], T.P2[:], ch, None, MUL, None, ["P2a", "cf"], ["TI1"])
-    op("v", lambda: V.transpose(T.TO[:], T.TI[:]), ["TI0", "TI1"], ["TO"])
-    for c in range(8):
-        tt(T.Wi[:, c:128:8], T.TO[:, c, 0:16], T.TO[:, c, 16:32], ADD, ["TO"], ["Wi%d" % c])
-    WI = ["Wi%d" % c for c in range(8)]
-    Li, Ri = T.LR[:, 0, :], T.LR[:, 1, :]
-    ts(Ri, T.Wi[:], 11, None, SHR, None, WI, ["Ri"])
-    ts(Li, T.Wi[:], M_ - 1, None, AND, None, WI, ["Li"])
-    ts(T.r0[:], Ri, float(M_), float(M_), A.is_ge, MUL, ["Ri"], ["r0"])
-    cp(T.lown[:], T.LR[:], ["Li", "Ri"], ["loL", "loR"])
-    tt(T.r0[:], T.r0[:], Ri, ADD, ["r0", "Ri"], ["r0"])
-    ts(T.lsend[:, 256:512], T.LR[:], float(M_), None, ADD, None, ["Li", "Ri"], ["ls1L", "ls1R"])
-    cp(T.lsend[:, 128:256], T.r0[:], ["r0"], ["ls0R"])
-    cp(T.lsend[:, 0:128], Li, ["Li"], ["ls0L"])
-    tt(T.ksend[:], T.lb[:], T.pv[:, 0:128], A.subtract, ["lb", "p:v"], ["ksend"])
-    ts(T.kown[:], T.ksend[:], -1.0, 0.5, MUL, ADD, ["ksend"], ["kown"])
 
-    before("g", ["ksend", "ls0L", "ls0R", "ls1L", "ls1R"], [])
-    used, tr = set(), []
-    for d in sorted(range(FAR), key=lambda d: not topo.may_write(core, dsts[d])):
-        direct = topo.may_write(core, dsts[d])
-        x = dsts[d] if direct else info_helper(hs_, d)
-        for src, dst in ((T.ksend[:], T.kin[:, 128 * d:128 * d + 128]), (T.lsend[:, 256 * d:256 * d + 256], T.lin[:, 256 * d:256 * d + 256])):
-            e = [y for y in topo.engines(core, x) if y not in used][:4]
-            used.update(e)
-            tr.append(RemoteDMATransfer(dst_ids=[dst_id(topo, x, core)], dma_engine_mask=bits(e),
-                                        remote_sem=T.sem.fari if direct else T.sem.arri, src=src, dst=dst))
-    g.remote_dma_fused(tr, local_sem=T.sem.sent)
-
-    before("g", ["hs"], [])
-    w = M_ // len(hs_)
-    g.remote_dma_fused([RemoteDMATransfer(dst_ids=[dst_id(topo, c, core)], dma_engine_mask=bits(topo.engines(core, c)[4 * i:4 * i + 4]),
-                                          remote_sem=T.sem.arrh, src=T.hs[:, i * w:(i + 1) * w], dst=T.HL[:, 0:w])
-                        for i, c in enumerate(hs_)], local_sem=T.sem.sent)
-    total["sent"] = 16 + 4 * len(hs_)
-    total["farh"], total["fari"] = 4 * FAR * len(hs_), 8 * FAR
-    wr["Hf"], wr["kin"], wr["lin"] = ("farh", None), ("fari", None), ("fari", None)
-    wins = [T.win0, T.win1, T.win2, T.win3]
-
-    before("s", ["kown"], IUO)
-    for f in (3, 7, 11):
-        dma("s", T.IU[f::16, OWN:TW], T.kown[:], "kown", ["kown"], ["IUok%d" % f])
-    for b in range(16, 24):
-        ur_blk(b)
-    before("s", [], URO)
-    for f in (7, 11):
-        dma("s", T.UR[f::16, OWN:TW], T.kown[:], "kowr", ["kown"], ["URok%d" % f])
-    IUO = IUO + ["IUok3", "IUok7", "IUok11", "IUp", "IUq"]
-    URO = URO + ["URok7", "URok11", "URq"]
-    for b in range(16):
-        ur_blk(b)
-
-    def kidb(q, dstT, name, lst, win, c0, n, R):
-        if q == "a":
-            act(dstT[:, c0:c0 + n], win.indirect(lst), AF.Copy, R, [name])
+    def digits(step, h):
+        c = slice(256 * h, 256 * h + 256)
+        if step == 0:
+            ts(T.Qi[:, c], T.pA[:, 0, c], C["qs"][0], C["qo"][0], MUL, ADD, ["p:A0", "c_qs", "c_qo"], ["Qi%d" % h])
+        elif step == 1:
+            ts(T.Qm[:, c], T.Qi[:, c], 255, None, AND, None, ["Qi%d" % h], ["Qm%d" % h])
         else:
-            cp(dstT[:, c0:c0 + n], win.indirect(lst), R, [name])
+            ts(T.Qb[:, c], T.Qm[:, c], C["qt"][0], C["qu"][0], MUL, ADD, ["Qm%d" % h, "c_qt", "c_qu"], ["Qb%d" % h])
 
-    HO = ["Ho0", "Ho1", "Hp", "Hq"]
-    kidb("a", T.HL, "HLo", T.lown[:, 0:128], T.H[:, OWN:TW + 16], OWN, 2048, HO + ["loL"])
-    kidb("a", T.HR, "HRo", T.lown[:, 128:256], T.H[:, OWN:TW + 16], OWN, 2048, HO + ["loR"])
+    digits(0, 0)
+    digits(0, 1)
+    tt(T.TI[:, :, 0:16], T.r0[:], T.ls[:], ADD, ["r0", "ls"], ["TI0"])
+    digits(1, 0)
+    digits(1, 1)
+    act(T.TI[:, :, 16:32], T.TI[:, :, 0:16], ["TI0"], ["TI1"])
+    digits(2, 0)
+    digits(2, 1)
+    banks = [(T.pB, 0, "p:B0"), (T.pB, 1, "p:B1"), (T.pC, 0, "p:C0"), (T.pC, 1, "p:C1")]
+    for P_, b, key in banks:
+        mm([(P_[:, b, 256 * h:256 * h + 256], T.Cm[0:65, :], T.XB[0:65, :]) for h in range(2)],
+           ["Cm0", "Cm9", "Cm73", "Cm74", "XB", "XB2"], [key], stop=False)
+    for i in range(4):
+        P_, b, key = banks[i]
+        mm([(P_[:, b, :], mx("G", 16 * i), T.Qb[:])], ["G%d" % i, "Qb0", "Qb1"], [key], start=False)
+    op("v", lambda: V.transpose(T.TO[:], T.TI[:]), ["TI0", "TI1"], ["TO"])
+    cp(T.Wi[:], T.TO[:].indirect(T.lo8[:]), ["TO", "lo8"], ["Wi"])
+    ts(T.Ri[:], T.Wi[:], 11, None, SHR, None, ["Wi"], ["Ri"])
+    ts(T.Li[:], T.Wi[:], M_ - 1, None, AND, None, ["Wi"], ["Li"])
+    ts(T.lown[:, 128:256], T.Ri[:], float(M_), None, A.min, None, ["Ri"], ["loR"])
+    cp(T.lown[:, 256:384], T.Li[:], ["Li"], ["loL"])
+    cp(T.lown[:, 0:128], T.Ri[:], ["Ri"], ["loQ"])
+    push(1, [(0, T.lown[:, 0:256])], ["loR", "loQ"])
+    for b8 in range(8):
+        P_, b, key = banks[b8 // 2]
+        src, out, kb = P_[:, b, 256 * (b8 % 2):256 * (b8 % 2) + 256], T.K[:, 256 * b8:256 * b8 + 256], T.KB[:, b8:b8 + 1]
+        if OPT["kp"][b8 // 2] == "v":
+            ts(out, src, kb, None, ADD, None, [key, "KB"], ["K%d" % b8])
+        else:
+            act(out, src, [key, "KB"], ["K%d" % b8], bias=kb)
+    KA = ["K%d" % b for b in range(8)] + ["Kp"]
 
-    def ix_a(lst, lo, hi, gc, n, R):
-        act(T.G[:, gc:gc + n], T.IU[:, lo:hi].indirect(lst), AF.Identity, R + ["ov"], ["G%d" % gc], scale=v0)
+    tb = [(T.pD, 0, "p:D0"), (T.pD, 1, "p:D1"), (T.pA, 0, "p:A0"), (T.pA, 1, "p:A1")]
 
-    def ix_v(lst, lo, hi, gc, c0, n, R):
-        tt(T.IX[:, c0:c0 + n], T.UR[:, lo:hi].indirect(lst), T.G[:, gc:gc + n], ADD, R + ["G%d" % gc], ["IX%d" % c0])
+    def t_self(i, bank, W3):
+        P_, b, key = bank
+        mm([(P_[:, b, :], mx(W3), T.K[:, 512 * i:512 * i + 512])], ["K%d" % (2 * i), "K%d" % (2 * i + 1), W3], [key], stop=False)
+
+    def t_mm(i, bank, W1, W2, R):
+        P_, b, key = bank
+        c = slice(512 * i, 512 * i + 512)
+        mm([(P_[:, b, :], W1, T.gL[:, c]), (P_[:, b, :], W2, T.gR[:, c])], R + ["gL%d" % i, "gR%d" % i], [key], start=False)
+
+    def t_pass(q, out, bank, bias, W):
+        P_, b, key = bank
+        if q == "v":
+            ts(out, P_[:, b, :], -1.0, C[bias][0], MUL, ADD, [key, C[bias][1]], W)
+        else:
+            act(out, P_[:, b, :], [key, C[bias][1]], W, scale=-1.0, bias=C[bias][0])
 
     for i in range(4):
-        ix_a(T.lown[:, 32 * i:32 * i + 32], OWN, TW + 16, 512 * i, 512, IUO + ["loL"])
-
-    ts(T.oer[:], T.xI[:, 0:4], ce, 3.0, ADD, EQ, ["xI", "cf"], ["oer"])
-    ts(chi, e3, 0.5 - 1e6, 1e6, MUL, ADD, ["oe"], ["chi"])
-    ts(cbm, v1, -256.0, 128.0, MUL, ADD, ["ov"], ["cbm"])
-    cp(cpf, p, ["pI"], ["cpf"])
-    ts(T.jI[:], T.jI[:], F_ - 1, None, AND, None, ["jI"], ["jI"])
-    op("v", lambda: V.tensor_tensor_scan(T.w1[:], T.c256[:], T.oer[:], 0.0, MUL, ADD), ["c256", "oer"], ["w1"])
-    op("v", lambda: V.tensor_tensor_scan(T.w0[:, 1:4], T.c256[:, 1:4], T.oer[:, 1:4], 0.0, MUL, ADD), ["c256", "oer"], ["w0"])
-    ts(T.Blk[:], T.ui[:], cg, None, EQ, None, ["ui", "cf"], ["Blk"])
-    ts(T.Idn[:], T.xI[:, 0:128], cpf, None, EQ, None, ["xI", "cpf"], ["Idn"])
-    cp(T.J0[:], T.jI[:], ["jI"], ["J0"])
-    ts(T.cj[:, 0:1], p, 15, None, AND, None, ["pI"], ["cj0"])
-    ts(T.cj[:, 1:2], p, 7, None, AND, None, ["pI"], ["cj1"])
-    ts(T.cj[:, 2:3], p, 3, 1, SHR, AND, ["pI"], ["cj2"])
-    tt(c2, c15, v2, ADD, ["c15", "ov"], ["c2"])
-    tt(c3, c15, v1, ADD, ["c15", "ov"], ["c3"])
-    cp(T.cq[:, 0:3], T.cj[:, 0:3], ["cj0", "cj1", "cj2"], ["cq"])
-    ts(cnz, v3, -1.0, 1.0, MUL, ADD, ["ov"], ["cnz"])
-    ts(T.B2[:], T.xI[:, 0:144], c2, None, EQ, None, ["xI", "c2"], ["B2"])
-    ts(T.B3[:], T.xI[:, 0:144], c3, None, EQ, None, ["xI", "c3"], ["B3"])
-    ts(cpm, cg, 8.0, T.cq[:, 1:2], MUL, ADD, ["cf", "cq"], ["cpm"])
-    ts(T.cq[:, 3:4], T.cq[:, 2:3], -1.0, 1.0, MUL, ADD, ["cq"], ["cq3"])
-    ts(T.JD[:], T.JC[:], T.cq[:, 0:1], 2048.0, ADD, ADD, ["JC", "cq"], ["JD"])
-    ts(T.JC[:], T.JC[:], T.cq[:, 0:1], None, ADD, None, ["JC", "cq"], ["JC"])
-    ts(T.PM0[:], T.uh[:], cpm, T.cq[:, 3:4], EQ, MUL, ["uh", "cpm", "cq3"], ["PM0"])
-    ts(T.PM1[:], T.uh[:], cpm, T.cq[:, 2:3], EQ, MUL, ["uh", "cpm", "cq"], ["PM1"])
-    ms(T.Z0[:], 0.0, ["Z0"])
-    w1, w0 = T.w1[:, 3:4], T.w0[:, 3:4]
-    for name, B, a_, b_ in (("WL", "B1", w1, v0), ("WE", "B3", w1, csg), ("WP", "B1", w1, v2), ("WC", "B1", w1, csg), ("WN", "B2", w1, cnz),
-                            ("WP0", "B1", w0, v2), ("WC0", "B1", w0, csg), ("WN0", "B2", w0, cnz)):
-        ts(T[name][:], T[B][:], a_, b_, MUL, MUL, [B, "w1", "w0", "ov", "csg", "cnz"], [name])
-    ts(T.BK[:], T.B1[:], 4096.0, None, MUL, None, ["B1"], ["BK"])
-    tt(T.ML[:], T.Blk[:], T.uf[:], MUL, ["Blk", "uf"], ["ML"])
-    tt(T.MR[:], T.Blk[:], T.ug[:], MUL, ["Blk", "ug"], ["MR"])
-    ts(T.AB[:, 0:16], T.SA[:], float(OWN), None, ADD, None, ["SA"], ["A0"])
-    cp(T.AB[:, 16:32], T.SB[:], ["SB"], ["B0"])
+        t_self(i, tb[i], "W3f")
     for i in range(4):
-        ix_v(T.lown[:, 128 + 32 * i:160 + 32 * i], OWN, TW + 16, 512 * i, OWN + 512 * i, 512, URO + ["loR"])
+        c = slice(512 * i, 512 * i + 512)
+        act(T.gL[:, c], T.K[:].indirect(T.lown[:, 256 + 32 * i:288 + 32 * i]), KA + ["loL"], ["gL%d" % i], scale=-1.0)
+        ts(T.gR[:, c], T.K[:].indirect(T.lown[:, 128 + 32 * i:160 + 32 * i]), -1.0, None, MUL, None, KA + ["loR"], ["gR%d" % i])
+        t_self(i, banks[i], "W3o")
+        t_mm(i, tb[i], mx("Ihi", 1), mx("Ihi"), ["Ihi"])
+    for i in range(4):
+        t_mm(i, banks[i], mx("Ilo", 1), mx("Ilo"), ["Ilo", "Ilo0"])
+    for i in range(4):
+        t_pass("av"[i % 2], T.Tf[:, 512 * i:512 * i + 512], tb[i], "bf", ["Tf%d" % i])
+        if i % 2:
+            push(2, [(j, T.Tf[:, 512 * j:512 * j + 512]) for j in (i - 1, i)], ["Tf%d" % (i - 1), "Tf%d" % i])
+    for q_, a_, b_ in OPT["lf"]:
+        (act if q_ == "a" else cp)(T.Lf[:, 256 * a_:256 * b_], T.hs[:].indirect(T.lown[:, 256 + 16 * a_:256 + 16 * b_]), ["hs", "loL"], ["Lf" + q_])
+    push(3, [(i, T.Lf[:, 512 * i:512 * i + 512]) for i in range(nh)], ["Lfa", "Lfv"])
+    dma("s", T.HL[0::2, 0:M_], T.Lf[1::2, :], "lhl", ["Lfa", "Lfv"], ["HLo0"])
+    dma("s", T.HL[1::2, 0:M_], T.Lf[0::2, :], "lhl", ["Lfa", "Lfv"], ["HLo1"])
+    fiota(T.H[:, GAP + 16:OWNU], [[0, OWNU - GAP - 16]], ["Hg"])
+    fiota(T.ga[:], [[0, 128]], ["ga"], base=2)
+    asel(T.gb[:], T.ga[:], [[-16, 8], [0, 16]], A.is_ge, 0.0, 0, 1, ["ga"], ["gb"])
+    asel(T.Blk2[:], T.gb[:], [[16, 8], [0, 16]], A.is_ge, 0.0, 15, -1, ["gb"], ["Blk2"])
+    asel(T.gb[:], T.Blk2[:], [[0, 8], [1, 16]], A.is_ge, 0.0, -8, 0, ["Blk2"], ["gb"])
+    asel(T.Tri2[:], T.Blk2[:], [[1, 128]], A.is_gt, 0.0, 0, -1, ["Blk2"], ["Tri2"])
+    fiota(T.ga[:], [[0, 128]], ["ga"], base=8192)
+    asel(T.Idn[:], T.ga[:], [[1, 128]], A.is_equal, 0.0, 0, -1, ["ga"], ["Idn"])
+    asel(T.TriL[:], T.Tri2[:], [[1, 128]], A.not_equal, -1.0, 0, -1, ["Tri2"], ["TriL"])
+    asel(T.Rst2[:], T.Blk2[:], [[-1, 128]], A.is_ge, 0.0, 0, 1, ["Blk2"], ["Rst2"])
+    asel(T.RstL[:], T.Rst2[:], [[1, 128]], A.not_equal, 3.0, 0, -1, ["Rst2"], ["RstL"])
+    fiota(T.JC[:], [[32, 64]], ["JC"], cm=2)
+    fiota(T.JD[:], [[16, 64]], ["JD"], base=DUMP, cm=1)
+    fiota(T.J0[:], [[2, 64]], ["J0"], cm=128)
+    wins = [T.win0, T.win1, T.win2, T.win3]
     for i, wn in enumerate(wins):
-        op("g", lambda: g.iota(wn[:, 0:1026], [[0, 1026]], 0, 0, allow_small_or_imprecise_dtypes=True), [], ["win%d" % i])
-    op("g", lambda: g.affine_select(T.Tri[:], T.Blk[:], [[1, 128]], A.is_gt, 0.0, 0, -1), ["Blk"], ["Tri"])
+        fiota(wn[:, 0:WZ], [[0, WZ]], ["win%d" % i])
 
-    before("s", ["kin"], IUF + URF)
-    for tab, keys, rows, s in (("IU", IUF, (3, 7, 11), "kfu"), ("UR", URF, (7, 11), "kfr")):
-        for f in rows:
-            for d in range(FAR):
-                dma("s", T[tab][f::16, M_ * d:M_ * d + M_], T.kin[:, 128 * d:128 * d + 128], s, ["kin"], ["%sk%d_%d" % (tab, d, f)])
-                keys.append("%sk%d_%d" % (tab, d, f))
-    IUA = IUF + IUO
-    IXA = ["IX%d" % c for c in range(0, PAD, 512)] + ["IX%d" % (OWN + 512 * i) for i in range(4)] + ["IXp"]
-    HA = HO + ["Hf"]
-    HLA = ["HLo", "HLp"] + ["HL%d" % i for i in range(8)]
-    HRA = ["HRo", "HRp"] + ["HR%d" % i for i in range(8)]
+    ts(T.Di[:, 0:16], T.SB[:], 31, None, AND, None, ["SB"], ["Di0"])
+    ts(T.Di[:, 16:32], T.SB[:], 5, None, SHR, None, ["SB"], ["Di1"])
+    ts(T.Di[:, 32:48], T.SB[:], 15, None, AND, None, ["SB"], ["Di2"])
+    ts(T.Di[:, 48:64], T.SB[:], 4, None, SHR, None, ["SB"], ["Di3"])
+    cp(T.AB[:, 0:16], T.SA[:], ["SA"], ["AB0"])
+    ts(T.D3[:, 0:16], T.Di[:, 0:16], 8.0, None, MUL, None, ["Di0"], ["D30"])
+    ts(T.D3[:, 16:32], T.Di[:, 16:32], 64.0, None, ADD, None, ["Di1"], ["D31"])
+    cp(T.AB[:, 32:64], T.Di[:, 32:64], ["Di2", "Di3"], ["AB2"])
+    cp(T.AB[:, 16:32], T.SB[:], ["SB"], ["AB1"])
 
-    def farl(i, right):
-        c = 256 * (i // 4) + 128 * right + 32 * (i % 4)
-        return T.lin[:, c:c + 32]
+    ms(T.H[:, UW:UW + 16], -262144.0, ["Hq"])
+    for c in cols:
+        lin(*c)
+    for i in range(4):
+        t_pass(OPT["to"][i], T.TX[:, 512 * i:512 * i + 512], banks[i], "bo", ["TXo%d" % i])
+    TO_ = ["TXo%d" % i for i in range(4)]
+    HO = ["Ho0", "Ho1"]
+    HA = HO + ["Hf", "Hg", "Hp", "Hq"]
+    act(T.St[:, 0:512], T.XB[:].indirect(T.D3[:, 0:32]), ["XB", "XB2", "D30", "D31", "c_sd"], ["St0"], scale=C["sd"][0])
+    act(T.St[:, 512:768], T.K[:].indirect(T.AB[:, 0:16]), KA + ["AB0"], ["St1"])
+    act(T.St[:, 768:1024], T.O16[:].indirect(T.AB[:, 32:48]), ["O16", "AB2"], ["St2"])
+    wu, ws, wt, U16 = MXO["WU"], MXO["WS"], MXO["WT"], T.X8[:, 0:128:8]
+    eqm(T.BK[:], xs(-15, 144), "xF", "g16", 8192.0, ["BK"])
+    eqm(T.MX[:, wu:wu + 16, 4], U16, "X8", "g16", None, ["WU"])
+    eqm(T.MX[:, ws:ws + 16:2, 4], xs(0, 8, 16), "xF", "g16", None, ["WS"])
+    eqm(T.tb[:], U16, "X8", "g16", "e7", ["tb"])
+    eqm(T.MX[:, wu:wu + 16, 5], U16, "X8", "g16", -1.0, ["WU"])
+    eqm(T.MX[:, ws:ws + 16:2, 3], xs(0, 8, 16), "xF", "g16", None, ["WS"])
+    eqm(T.tc[:], U16, "X8", "g16", "e15", ["tc"])
+    for name, m_, e_ in (("WCL", "r0", "e3"), ("WCR", "r2", "e11")):
+        eqm(mx(name), T.X8[:], "X8", "t8", m_, [name])
+    eqm(mx("WT"), xs(0, 128), "xF", "p", "m4", ["WT"])
+    eqm(T.ta[:], xs(0, 16, 8), "xF", "y8", "u", ["ta"])
+    for name, m_, e_ in (("WCL", "r0", "e3"), ("WCR", "r2", "e11")):
+        ts(T.MX[:, MXO[name]:MXO[name] + 16, 4:6], T.MX[:, wu:wu + 16, 4:6], C[e_][0], None, MUL, None, ["WU", "O16"], [name])
+    tt(T.MX[:, wt:wt + 16, 4], T.tb[:], T.ta[:], ADD, ["ta", "tb"], ["WT"])
+    eqm(T.WC[:], xs(-15, 144), "xF", "g16", "wL", ["WC"])
+    tt(T.MX[:, wt:wt + 16, 5], T.tc[:], T.ta[:], A.subtract, ["ta", "tc"], ["WT"])
+    late = [[lambda: eqm(T.WN[:], xs(-15, 144), "xF", "c2", "w", ["WN"]),
+             lambda: eqm(T.WR[:], xs(-15, 144), "xF", "g16", "wR", ["WR"]),
+             lambda: ms(T.kk[:, :, 0:66:65], 0.0, ["kk0"]),
+             lambda: ms(T.T2[:, 0:66:65], 0.0, ["T20"])],
+            [lambda: ts(T.WM[:], T.gb[:], -float(2 ** 24), None, MUL, None, ["gb"], ["WM"])]]
 
-    def kid(q, i, right):
-        return lambda: kidb(q, T.HR if right else T.HL, ("HR%d" if right else "HL%d") % i, farl(i, right), T.H[:, 0:OWN], 512 * i, 512, ["Hf", "Hp", "lin"])
+    def kid(q, i, n):
+        t, c = i // 8, 16 * (i % 8)
+        if t == 0:
+            win, lst, R = T.H[:, OWNU:UW + 16], T.lown[:, 128 + c:128 + c + 16 * n], HO + ["Hq", "loR"]
+        else:
+            c += 128 * (t - 1)
+            win, lst, R = T.H[:, M_ * (t - 1):GAP + 16], T.lin[:, c:c + 16 * n], ["Hf", "Hp", "lin"]
+        (act if q == "a" else cp)(T.HR[:, 256 * i:256 * (i + n)], win.indirect(lst), R, ["HR%d" % j for j in range(i, i + n)])
 
-    hra = OPT["hra"]
-    fill_a = [lambda i=i: ix_a(farl(i, 0), 0, OWN, 512 * i, 512, IUF + ["IUp", "lin"]) for i in range(8)]
-    fill_v = [lambda i=i: ix_v(farl(i, 1), 0, OWN, 512 * i, 512 * i, 512, URF + ["URp", "lin"]) for i in range(8)]
-    fill_a += [kid("a", i, 0) for i in range(8)] + [kid("a", i, 1) for i in range(8 - hra, 8)]
-    fill_v += [kid("v", i, 1) for i in range(8 - hra)]
+    done = [0]
 
     def fill(na, nv):
-        for _ in range(na):
-            if fill_a:
-                fill_a.pop(0)()
-        for _ in range(nv):
-            if fill_v:
-                fill_v.pop(0)()
+        for q, n in (("a", na), ("v", nv)):
+            while n and done[0] < 24:
+                m = min(n, 8 - done[0] % 8)
+                kid(q, done[0], m)
+                done[0] += m
+                n -= m
 
-    def decode(parts, k, c0):
-        big = float(OWN + PAD)
-        for C, key, sl in parts:
-            cp(T.Ci[:, sl], C, [key], ["Ci%d" % sl.start])
-        for C, key, sl in parts:
-            ts(T.tU[:, sl], C, float(2 ** 23), big, A.is_lt, MUL, [key], ["tU%d" % sl.start])
-        ts(T.ai[:, 0:k], T.Ci[:, 0:k], M_ - 1, None, AND, None, ["Ci0", "Ci1"], ["ai"])
-        ts(T.bi[:, 0:k], T.Ci[:, 0:k], 11, FAR * M_ - 1, SHR, AND, ["Ci0", "Ci1"], ["bi"])
-        tt(T.zU[:, 0:k], T.ai[:, 0:k], T.tU[:, 0:k], ADD, ["ai", "tU0", "tU1"], ["zU"])
-        ts(T.b4[:, 0:k], T.bi[:, 0:k], float(PAD), None, ADD, None, ["bi"], ["b4"])
-        ts(T.tX[:, 0:k], T.tU[:, 0:k], -1.0, big, MUL, ADD, ["tU0", "tU1"], ["tX"])
-        tt(T.Uf[:, 0:k], T.zU[:, 0:k], T.b4[:, 0:k], A.max, ["zU", "b4"], ["Uf"])
-        tt(T.zX[:, 0:k], T.ai[:, 0:k], T.tX[:, 0:k], ADD, ["ai", "tX"], ["zX"])
-        ts(T.UO[:, c0:c0 + k], T.Uf[:, 0:k], -float(PAD), None, ADD, None, ["Uf"], ["U%d" % c0])
-        tt(T.Xf[:, 0:k], T.zX[:, 0:k], T.b4[:, 0:k], A.max, ["zX", "b4"], ["Xf"])
-        ts(T.XO[:, c0:c0 + k], T.Xf[:, 0:k], -float(PAD), None, ADD, None, ["Xf"], ["X%d" % c0])
-
-    def clamp(lo, hi):
-        ts(T.Mc[:, lo:hi], T.Mb[:, lo:hi], 0.0, chi, A.max, A.min, ["Mb%d" % lo, "chi"], ["Mc%d" % lo])
-
+    TA = TO_ + ["TXf"]
+    HLA = ["HLo0", "HLo1", "HLf"]
+    HRA = ["HR%d" % i for i in range(24)]
     f = OPT["f"]
-    VW = ((T.pv, "p:v"), (T.pw, "p:w"))
-    act(T.GU[:, 0:256], T.IU[:].indirect(T.AB[:, 0:16]), AF.Copy, IUA + ["A0"], ["GU"])
-    fill(f[0], f[1])
-    tt(T.Mb[:, 0:256], T.IU[:].indirect(T.AB[:, 16:32]), T.GU[:, 0:256], ADD, IUA + ["B0", "GU"], ["Mb0"])
-    clamp(0, 256)
-    mm([(T.pv[:, 0:16], sel(T.WL, s), T.Mc[:, s:256:16]) for s in range(16)], ["WL", "Mc0"], ["p:v"])
-    fill(f[2], f[3])
-    decode([(T.pv[:, 0:16], "p:v", slice(0, 16))], 16, 0)
 
-    def expand(k, c0, pa, pv_, na, nv):
-        n = 16 * k
-        act(T.GU[:, 0:n], T.IU[:].indirect(T.UO[:, c0:c0 + k]), AF.Copy, IUA + ["U%d" % c0], ["GU"])
-        fill(pa + na, pv_)
-        tt(T.Mb[:, 0:n], T.IX[:].indirect(T.XO[:, c0:c0 + k]), T.GU[:, 0:n], ADD, IXA + ["X%d" % c0, "GU"], ["Mb0"])
-        clamp(0, n)
-        for h, (P_, key) in enumerate(VW):
-            mm([(P_[:, 0:k], sel(T.WE, 2 * s), T.Mc[:, 8 * h + s:n:16]) for s in range(8)], ["WE", "Mc0"], [key])
-        fill(0, nv)
-        decode([(T.pv[:, 0:k], "p:v", slice(0, 2 * k, 2)), (T.pw[:, 0:k], "p:w", slice(1, 2 * k, 2))], 2 * k, c0 + k)
+    def decode(k, c0):
+        cp(T.Ci[:, 0:k], T.pD[:, 0, 0:k], ["p:D0"], ["Ci"])
+        ts(T.ai[:, 0:k], T.Ci[:, 0:k], M_ - 1, None, AND, None, ["Ci"], ["ai"])
+        ts(T.bi[:, 0:k], T.Ci[:, 0:k], 11, None, SAR, None, ["Ci"], ["bi"])
+        tt(T.mn[:, 0:k], T.ai[:, 0:k], T.bi[:, 0:k], A.min, ["ai", "bi"], ["mn"])
+        ts(T.UO[:, c0:c0 + k], T.mn[:, 0:k], float(OWNU), None, ADD, None, ["mn"], ["U%d" % c0])
+        tt(T.mx[:, 0:k], T.ai[:, 0:k], T.bi[:, 0:k], A.max, ["ai", "bi"], ["mx"])
+        cp(T.XO[:, c0:c0 + k], T.mx[:, 0:k], ["mx"], ["X%d" % c0])
 
-    expand(16, 0, f[4], f[5], f[6], f[7])
-    expand(32, 16, 0, f[8], f[9], f[10])
-    fill(20, 20)
+    def clamp(out, src, chi, R, W):
+        ts(out, src, 0.0, C[chi][0], A.max, A.min, R + [C[chi][1]], W)
 
-    act(T.nU[:, 1024:1792], T.H[:].indirect(T.UO[:, 0:48]), AF.Identity, HA + ["U0", "U16"], ["nUe"], scale=-1.0)
-    tt(T.VL[:, 1024:1792], T.HL[:].indirect(T.XO[:, 0:48]), T.nU[:, 1024:1792], A.is_lt, HLA + ["X0", "X16", "nUe"], ["VLe"])
-    tt(T.VR[:, 1024:1792], T.HR[:].indirect(T.XO[:, 0:48]), T.nU[:, 1024:1792], A.is_lt, HRA + ["X0", "X16", "nUe"], ["VRe"])
-    for h in range(2):
-        mm([(T.pm[:, h, 0:48], sel(T.BK, 2 * s + e), Vb[:, 1024 + 8 * h + s:1792:16]) for e, Vb in ((0, T.VL), (1, T.VR)) for s in range(8)],
-           ["BK", "VLe", "VRe"], ["p:m%d" % h])
+    fill(f[0], 8 - f[0])
+    o = T.pA[:, 0, 0:256]
+    mm([(o, sel(T.BK, 1 + e), T.St[:, 256 * e:256 * e + 256]) for e in range(2)] + [(o, mx("WT"), T.St[:, 512:768]), (o, mx("WU"), T.St[:, 768:1024])],
+       ["BK", "WT", "WU", "St0", "St1", "St2"], ["p:A0"], stop=False)
+    for f_ in late[0]:
+        f_()
+    act(T.St[:, 1280:1536], T.H[:, 0:GAP].indirect(T.AB[:, 16:32]), ["Hf", "AB1"], ["St3"], scale=-1.0)
+    mm([(o, mx("WU"), T.St[:, 1280:1536])], ["St3"], ["p:A0"], start=False, stop=False)
+    ts(T.LF[:], T.lin[:, 0:256], float(M_), BIG, A.is_ge, MUL, ["lin"], ["LF"])
+    tt(T.St[:, 1536:1792], T.LF[:].indirect(T.AB[:, 48:64]), T.St[:, 768:1024], MUL, ["LF", "AB2", "St2"], ["St4"])
+    mm([(o, mx("WS"), T.St[:, 1536:1792])], ["WS", "St4"], ["p:A0"], start=False)
+    fill(f[1], f[2])
+    clamp(T.P0[:], o, "ch0", ["p:A0"], ["P0"])
+    mm([(T.pD[:, 0, 0:16], sel(T.WC, s), T.P0[:, s:256:16]) for s in range(16)], ["WC", "P0"], ["p:D0"])
+    mm([(o, mx("WCL"), T.P0[:])], ["WCL", "P0"], ["p:A0"], stop=False)
+    fill(0, f[3])
+    decode(16, 0)
 
-    def early_d2():
-        for h in range(2):
-            cp(T.d2[:, h:32:2], T.pm[:, h, 0:16], ["p:m%d" % h], ["d2%d" % h])
-        for h, (P_, key) in enumerate(VW):
-            mm([(P_[:, 0:32], T["PM%d" % h][:], T.d2[:])], ["PM%d" % h, "d20", "d21"], [key])
-            cp(T.d3[:, 32 * h:32 * h + 32], T.pm[:, h, 16:48], ["p:m%d" % h], ["d3%d" % h])
+    act(T.nU[:, 1024:1280], T.H[:].indirect(T.UO[:, 0:16]), HA + ["U0"], ["nUa"], scale=-1.0)
+    cp(T.Tg[:, 0:256], T.TX[:].indirect(T.XO[:, 0:16]), TA + ["X0"], ["Tg0"])
+    mm([(o, mx("WU"), T.nU[:, 1024:1280])], ["nUa"], ["p:A0"], start=False, stop=False)
+    mm([(o, mx("WT"), T.Tg[:, 0:256])], ["WT", "Tg0"], ["p:A0"], start=False)
+    VE = (T.VL, T.VR)
 
-    def early_dead():
-        for h, (P_, key) in enumerate(VW):
-            tt(T.dead[:, h:64:2], P_[:, 0:32], T.d3[:, 32 * h:32 * h + 32], ADD, [key, "d3%d" % h], ["dead%d" % h])
+    def early(at):
+        for e, a_, b_ in OPT["early"][at]:
+            lo, hi = 1024 + 256 * a_, 1024 + 256 * b_
+            tt(VE[e][:, lo:hi], (T.HL, T.HR)[e][:].indirect(T.XO[:, 16 * a_:16 * b_]), T.nU[:, lo:hi], A.is_lt,
+               (HLA, HRA)[e] + ["X0", "nUa"] + (["X16", "nUb"] if b_ > 1 else []), ["Ve%d%d" % (e, j) for j in range(a_, b_)])
 
-    cuts, mc = OPT["cuts"], OPT["mc"]
+    fill(f[4], f[5])
+    early(0)
+    clamp(T.P1[:], o, "ch", ["p:A0"], ["P1"])
+    mm([(T.pD[:, 0, 0:32], sel(T.WN, 2 * q_), T.P1[:, q_:256:8]) for q_ in range(8)], ["WN", "P1"], ["p:D0"])
+    WE = (mx("WCL"), mx("WCR"))
+    for e in range(2):
+        mm([(T.pA[:, e, 0:256], WE[e], T.P1[:])], ["WCL", "WCR", "P1"], ["p:A%d" % e], stop=False)
+    for f_ in late[1]:
+        f_()
+    decode(32, 16)
+    act(T.nU[:, 1280:1792], T.H[:].indirect(T.UO[:, 16:48]), HA + ["U16"], ["nUb"], scale=-1.0)
+    cp(T.Tg[:, 0:512], T.TX[:].indirect(T.XO[:, 16:48]), TA + ["X16"], ["Tg0"])
+    for e in range(2):
+        mm([(T.pA[:, e, 0:256], mx("WU"), T.nU[:, 1280 + e:1792:2])], ["nUb"], ["p:A%d" % e], start=False, stop=False)
+    for e in range(2):
+        mm([(T.pA[:, e, 0:256], mx("WT"), T.Tg[:, e:512:2])], ["Tg0"], ["p:A%d" % e], start=False)
+    fill(f[6], f[7])
+    early(1)
+    for e in range(2):
+        clamp(T.P2[:, e:512:2], T.pA[:, e, 0:256], "ch", ["p:A%d" % e], ["P2%d" % e])
+    mm([(T.pD[:, 0, 0:64], sel(T.WN, 2 * q_), T.P2[:, q_:512:8]) for q_ in range(8)], ["WN", "P20", "P21"], ["p:D0"])
+    for e in range(2):
+        mm([(T.pA[:, e, :], WE[e], T.P2[:])], ["P20", "P21"], ["p:A%d" % e], stop=False)
+    fill(f[8], f[9])
+    early(2)
+    decode(64, 48)
+    fill(f[10], f[11])
+    early(3)
+
+    cuts = OPT["cuts"]
     nc = len(cuts) - 1
-    VLK, NU, DK = ["VL%d" % i for i in range(nc)], ["nU%d" % i for i in range(nc)], ["dead0", "dead1"]
-
-    def mask_l(i):
-        mm([(T.pm[:, i, :], T.ML[:], T.VL[:, 512 * i:512 * i + 512])], ["ML"] + VLK, ["p:m%d" % i], stop=False)
-
-    def mask_r(i):
-        mm([(T.pm[:, i, :], T.MR[:], T.VR[:, 512 * i:512 * i + 512])], ["MR", "VR", "VR0"], ["p:m%d" % i], start=False)
-        act(T.mk[:, 512 * i:512 * i + 512], T.pm[:, i, :], AF.Sigmoid, ["p:m%d" % i, "cbm"], ["mk%d" % i], bias=cbm, scale=256.0)
-
+    VLK, VRK, NU = ["VL%d" % i for i in range(nc)], ["VR%d" % i for i in range(nc)], ["nU%d" % i for i in range(nc)]
     for r in range(4):
         last = r == 3
         c0 = 48 + 64 * r
         xk, uk = "X%d" % c0, "U%d" % c0
         wn, wk = wins[r], "win%d" % r
-
-        def test(Vb, tab, a_, b_, R, W):
-            tt(Vb[:, 16 * a_:16 * b_], tab[:].indirect(T.XO[:, c0 + a_:c0 + b_]), T.nU[:, 16 * a_:16 * b_], A.is_lt, R + [xk], W)
-
-        def mpart(lo, hi):
-            tt(T.Mb[:, lo:hi], T.IX[:].indirect(T.XO[:, c0 + lo // 16:c0 + hi // 16]), T.GU[:, lo:hi], ADD, IXA + [xk, "GU"], ["Mb%d" % lo])
-
+        part = (lambda t, h: t[:, h:1024:2]) if r == 0 else (lambda t, h: t[:, 512 * h:512 * h + 512])
         for i in range(nc):
             a_, b_ = cuts[i], cuts[i + 1]
-            act(T.nU[:, 16 * a_:16 * b_], T.H[:].indirect(T.UO[:, c0 + a_:c0 + b_]), AF.Identity, HA + [uk], ["nU%d" % i], scale=-1.0)
-        act(T.GU[:], T.IU[:].indirect(T.UO[:, c0:c0 + 64]), AF.Copy, IUA + [uk], ["GU"])
-        for i in range(nc):
-            test(T.VL, T.HL, cuts[i], cuts[i + 1], HLA + ["nU%d" % i], ["VL%d" % i])
-            if i == 0:
-                test(T.VR, T.HR, 0, cuts[1], HRA + ["nU0"], ["VR0"])
-            if r == 0 and i == nc - 2:
-                early_d2()
-            if r == 0 and i == nc - 1:
-                early_dead()
-        mm([(T.pc[:, 0, 0:64], T.Idn[:], T.dead[:])] + [(T.pc[:, 0, 0:64], sel(T.BK, s), T.VL[:, s:1024:16]) for s in range(16)],
-           ["Idn", "BK"] + DK + VLK, ["p:c0"])
-        mask_l(0)
-        test(T.VR, T.HR, cuts[1], 64, HRA + NU, ["VR"])
-        mm([(T.pc[:, 1, 0:64], T.Idn[:], T.dead[:])] + [(T.pc[:, 1, 0:64], sel(T.BK, s), T.VR[:, s:1024:16]) for s in range(16)],
-           ["Idn", "BK", "VR", "VR0"] + DK, ["p:c1"])
-        mask_r(0)
-        tt(T.T1[:], T.pc[:, 0, 0:64], T.JD[:], A.min, ["p:c0", "JD"], ["T1"])
-        mpart(0, mc)
-        ts(T.kk[:], T.pc[:, :, 0:64], 0.0, None, EQ, None, ["p:c0", "p:c1"], ["kk"])
-        mm([(T.pt[:, 0:64], T.Blk[:], T.kk[:, e, :]) for e in range(2)], ["Blk", "kk"], ["p:t"])
-        mm([(T.pb[:, 0:64], T.Tri[:], T.kk[:, e, :]) for e in range(2)], ["Tri", "kk"], ["p:b"])
-        mask_l(1)
-        mask_r(1)
-        tt(T.T2[:], T.pc[:, 1, 0:64], T.T1[:], A.min, ["p:c1", "T1"], ["T2"])
-        mpart(mc, 1024)
-        op("v", lambda: V.tensor_tensor_scan(T.S[:, 1:65], T.pt[:, 0:64], T.Z0[:], 0.0, ADD, ADD), ["p:t", "Z0"], ["S"])
-        tt(T.O2[:], T.pb[:, 0:64], T.T2[:], ADD, ["p:b", "T2"], ["O2"])
-        if not last:
-            clamp(0, mc)
-        tt(T.O[:], T.S[:, 0:64], T.O2[:], ADD, ["S", "S0", "O2"], ["O"])
-        if not last:
-            clamp(mc, 1024)
-        ts(T.off[:], T.O[:], 1.0, None, ADD, None, ["O"], ["off"])
-        src, sk = (T.Mb, "Mb") if last else (T.Mc, "Mc")
-        tt(wn[:].indirect(T.off[:]), src[:], T.mk[:], MUL, ["off", sk + "0", sk + str(mc), "mk0", "mk1"], [wk])
-        cur, prv, both = ("WC0", "WP0", "WN0") if last else ("WC", "WP", "WN")
-        P_, key = VW[last]
-        mm([(P_[:, 0:64], sel(T[both if s < 15 else cur], s), wn[:, 1 + s:1010 + s:16]) for s in range(16)]
-           + [(P_[:, 0:64], sel(T[prv], 0), wn[:, 0:1009:16])], [cur, prv, both, wk], [key])
-        if not last:
-            ts(T.dead[:], T.JC[:], T.S[:, 64:65], 4096.0, A.is_ge, MUL, ["JC", "S"], DK)
-            decode([(T.pv[:, 0:64], "p:v", slice(0, 64))], 64, c0 + 64)
+            act(T.nU[:, 16 * a_:16 * b_], T.H[:].indirect(T.UO[:, c0 + a_:c0 + b_]), HA + [uk], ["nU%d" % i], scale=-1.0)
+        for h in range(2):
+            act(T.Tg[:, 512 * h:512 * h + 512], T.TX[:].indirect(T.XO[:, c0 + 32 * h:c0 + 32 * h + 32]), TA + [xk], ["Tg%d" % h])
 
-    mm([(T.pv[:, 0:64], sel(T[x], s), wn[:, o + 64 * s:o + 64 * s + 64]) for s in range(16) for x, o in ((cur, 1), (prv, 0))],
-       [cur, prv, wk], ["p:v"])
-    ts(T.df[:], T.J0[:], T.S[:, 64:65], None, A.is_ge, None, ["J0", "S"], ["df"])
-    ts(T.al[:], T.J0[:], T.S[:, 64:65], None, A.is_lt, None, ["J0", "S"], ["al"])
+        def failed(e):
+            mm([(T.pC[:, 0, 0:64], sel(T.BK, 4 * q_ + 2 * e + u), VE[e][:, 1024 + q_:1280:4]) for q_ in range(4) for u in range(2)]
+               + [(T.pC[:, 0, 0:64], sel(T.BK, 2 * q_ + e), VE[e][:, 1280 + q_:1792:8]) for q_ in range(8)],
+               ["BK"] + ["Ve%d%d" % (e, j) for j in range(3)], ["p:C0"], start=e == 1, stop=e == 0)
 
-    def split(C, key):
-        cp(T.Ci[:], C, [key], ["Ci0"])
-        ts(T.ai[:], T.Ci[:], M_ - 1, None, AND, None, ["Ci0"], ["ai"])
-        ts(T.bi[:], T.Ci[:], 11, None, SHR, None, ["Ci0"], ["bi"])
+        def test(e, i):
+            a_, b_ = cuts[i], cuts[i + 1]
+            tt(VE[e][:, 16 * a_:16 * b_], (T.HL, T.HR)[e][:].indirect(T.XO[:, c0 + a_:c0 + b_]), T.nU[:, 16 * a_:16 * b_], A.is_lt,
+               (HLA, HRA)[e] + [xk, "nU%d" % i], [("VL%d", "VR%d")[e] % i])
 
-    split(T.pw[:, 0:64], "p:w")
-    ts(T.FA[:, 0:64], T.ai[:], float(OWN), None, ADD, None, ["ai"], ["FA"])
-    cp(T.FA[:, 64:128], T.bi[:], ["bi"], ["FB"])
+        def pay(h, W_, src, keys, stop=False):
+            keys = keys if r == 0 or h == 1 else keys[:-1]
+            mm([(T.pA[:, h, :], T.WM[:] if W_ == "WM" else mx(W_), part(src, h))], [W_] + keys, ["p:A%d" % h], start=False, stop=stop)
+
+        def count(e):
+            mm([(T.pB[:, e, 0:64], T.Idn[:], T.dead[:])] + [(T.pB[:, e, 0:64], sel(T.BK, s), VE[e][:, s:1024:16]) for s in range(16)],
+               ["Idn", "BK", "dead"] + (VLK, VRK)[e], ["p:B%d" % e])
+
+        TG = ["Tg0", "Tg1"]
+        if r == 0:
+            failed(1)
+            for i in range(nc):
+                test(1, i)
+            early(4)
+            for W_, src, keys in (("WU", T.nU, NU), ("WM", T.VR, VRK)):
+                for h in range(2):
+                    pay(h, W_, src, keys)
+            failed(0)
+            test(0, 0)
+            test(0, 1)
+            cp(T.dead[:], T.pC[:, 0, 0:64], ["p:C0"], ["dead"])
+            test(0, 2)
+            pay(0, "WT", T.Tg, TG, True)
+            pay(1, "WT", T.Tg, TG, True)
+            count(1)
+            count(0)
+        else:
+            for i in range(nc):
+                test(1, i)
+                test(0, i)
+            pay(0, "WU", T.nU, NU)
+            pay(0, "WM", T.VR, VRK)
+            pay(1, "WU", T.nU, NU)
+            pay(0, "WT", T.Tg, TG, True)
+            pay(1, "WM", T.VR, VRK)
+            count(1)
+            pay(1, "WT", T.Tg, TG, True)
+            count(0)
+        chi = "chF" if last else "ch"
+
+        def top(at):
+            if OPT["c1"] == at:
+                ts(part(T.Mc, 1), T.Mb[:], C[chi][0], None, A.min, None, ["Mb", C[chi][1]], ["Mc1"])
+
+        act(T.Mb[:], T.pA[:, 1, :], ["p:A1"], ["Mb"], f=AF.Relu)
+        clamp(part(T.Mc, 0), T.pA[:, 0, :], chi, ["p:A0"], ["Mc0"])
+        tt(T.T1[:], T.pB[:, 1, 0:64], T.JD[:], A.min, ["p:B1", "JD"], ["T1"])
+        top(0)
+        ts(T.kk[:, :, 1:65], T.pB[:, :, 0:64], 0.0, None, EQ, None, ["p:B0", "p:B1"], ["kk"])
+        mm([(T.pC[:, 1, 0:65], T[W_][:], T.kk[:, e, u:u + 65]) for W_, e, u in (("RstL", 0, 0), ("TriL", 0, 1), ("Rst2", 1, 0), ("Tri2", 1, 1))],
+           ["RstL", "Rst2", "TriL", "Tri2", "kk", "kk0"], ["p:C1"])
+        tt(T.T2[:, 1:65], T.pB[:, 0, 0:64], T.T1[:], A.min, ["p:B0", "T1"], ["T2"])
+        top(1)
+        tt(T.dT[:, 0:65], T.T2[:, 1:66], T.T2[:, 0:65], A.subtract, ["T2", "T20"], ["dT"])
+        top(2)
+        op("v", lambda: V.tensor_tensor_scan(T.S[:, 0:65], T.pC[:, 1, 0:65], T.dT[:, 0:65], 0.0, ADD, ADD), ["p:C1", "dT"], ["S"])
+        top(3)
+        ts(T.off[:], T.S[:, 0:64], 3.0, None, ADD, None, ["S"], ["off"])
+        cp(wn[:].indirect(T.off[:]), T.Mc[:], ["off", "Mc0", "Mc1"], [wk])
+        b = int(last)
+        mm([(T.pD[:, b, 0:64], sel(T.WN if s < 15 else T.WC, s), wn[:, 2 + 2 * s:2019 + 2 * s:32]) for s in range(16)]
+           + [(T.pD[:, b, 0:64], sel(T.WR, s), wn[:, 3 + 2 * s:2020 + 2 * s:32]) for s in range(16)]
+           + [(T.pD[:, b, 0:64], sel(T.WR, 0), wn[:, 0:2017:32])], ["WN", "WC", "WR", wk], ["p:D%d" % b])
+        if not last:
+            ts(T.dead[:], T.JC[:], C["g32"][0], T.S[:, 64:65], A.subtract, A.is_ge, ["JC", "c_g32", "S"], ["dead"])
+            for h in range(2):
+                mm([(T.pA[:, h, :], WE[e], wn[:, 1024 * h + o_:1024 * h + o_ + 1023:2]) for e, o_ in ((0, 2), (1, 3), (1, 0))],
+                   [wk], ["p:A%d" % h], stop=False)
+            decode(64, c0 + 64)
+
+    mm([(T.pD[:, 0, 0:64], sel(W_, s), wn[:, o_ + 128 * s:o_ + 128 * s + 127:2]) for s in range(16) for W_, o_ in ((T.WC, 2), (T.WR, 3), (T.WR, 0))],
+       [wk], ["p:D0"])
+    ts(T.df[:], T.J0[:], C["g2k"][0], T.S[:, 64:65], A.subtract, A.is_ge, ["J0", "c_g2k", "S"], ["df"])
+    ts(T.al[:], T.df[:], -1.0 / 8192, 1.0 / 8192, MUL, ADD, ["df"], ["al"])
+    ts(T.dg[:], T.df[:], 1.0 - M_, float(M_), MUL, ADD, ["df"], ["dg"])
+
+    def split(b):
+        cp(T.Ci[:], T.pD[:, b, 0:64], ["p:D%d" % b], ["Ci"])
+        ts(T.ai[:], T.Ci[:], M_ - 1, None, AND, None, ["Ci"], ["ai"])
+        ts(T.bi[:], T.Ci[:], 11, None, SHR, None, ["Ci"], ["bi"])
+
+    split(1)
+    ts(T.FA[:, 0:64], T.ai[:], float(OWNU), None, ADD, None, ["ai"], ["FA"])
+    ts(T.FA[:, 64:128], T.bi[:], -float(M_), None, ADD, None, ["bi"], ["FB"])
     fc = OPT["fc"]
-    for i in range(len(fc) - 1):
-        a_, b_ = fc[i], fc[i + 1]
-        act(T.VL[:, 64 * a_:64 * b_], T.H[:].indirect(T.FA[:, 4 * a_:4 * b_]), AF.Copy, HA + ["FA"], VLK if i == 0 else ["fl%d" % i])
-        cp(T.VR[:, 64 * a_:64 * b_], T.H[:].indirect(T.FA[:, 64 + 4 * a_:64 + 4 * b_]), HA + ["FB"], ["VR", "VR0"] if i == 0 else ["fr%d" % i])
-        mm([(T.pc[:, 0, 0:64], sel(T.B1, s), Vb[:, 64 * s:64 * s + 64]) for Vb in (T.VL, T.VR) for s in range(a_, b_)],
-           ["B1", "VL0", "VR", "fl%d" % i, "fr%d" % i], ["p:c0"], start=i == 0, stop=i == len(fc) - 2)
-    split(T.pv[:, 0:64], "p:v")
+    for i, (q_, a_, b_) in enumerate(fc):
+        (act if q_ == "a" else cp)(T.gL[:, 64 * a_:64 * b_], T.H[:].indirect(T.FA[:, 4 * a_:4 * b_]), HA + ["FA", "FB"][a_ // 16:(b_ + 15) // 16], ["fs%d" % i])
+        mm([(T.pB[:, 0, 0:64], sel(T.BK, s % 16), T.gL[:, 64 * s:64 * s + 64]) for s in range(a_, b_)],
+           ["BK", "fs%d" % i], ["p:B0"], start=i == 0, stop=i == len(fc) - 1)
+    split(0)
     tt(T.oa[:], T.ai[:], T.df[:], A.subtract, ["ai", "df"], ["oa"])
-    tt(T.ob[:], T.bi[:], T.df[:], A.subtract, ["bi", "df"], ["ob"])
+    tt(T.ob[:], T.bi[:], T.dg[:], A.subtract, ["bi", "dg"], ["ob"])
     dma("s", T.ya[:], T.oa[:], "outs", ["oa"], [])
-    dma("a", T.yb[:], T.ob[:], "outs", ["ob"], [])
-    tt(T.oz[:], T.pc[:, 0, 0:64], T.al[:], MUL, ["p:c0", "al"], ["oz"])
-    dma("s", T.ys[:], T.oz[:], "outs", ["oz"], [])
+    dma("s", T.yb[:], T.ob[:], "outs", ["ob"], [])
+    tt(T.oz[:], T.pB[:, 0, 0:64], T.al[:], MUL, ["p:B0", "al"], ["oz"])
+    dma("a", T.ys[:], T.oz[:], "outs", ["oz"], [])
     for s in sorted(total, key=lambda s: s == "outs"):
         if max(seen[q].get(s, 0) for q in Q) < total[s]:
             g.wait_ge(T.sem[s], total[s])

from concourse.bass import DstId, RemoteDMATransfer
from concourse.mybir import AluOpType as A, ActivationFunctionType as AF

M_, FAR, F_ = 2048, 2, 1024
XW, GAP, OWNU, UW = 6144, 4096, 6144, 8192
DUMP, WW, WZ = 4100, 9344, 2064
BIG, MM = float(2 ** 22), float(2 ** 23)
KX = 48 + 64 * 4
OPT = {"cuts": [0, 12, 32, 64], "fc": [("a", 0, 10), ("v", 18, 32), ("a", 10, 18)], "c1": 2,
       "f": [4, 7, 1, 2, 6, 0, 0, 0, 0, 0, 0, 99], "to": "vava", "lin": 24, "kp": "aaav",
       "early": [[], [], [(1, 0, 1)], [(1, 1, 3)], [(0, 0, 3)]], "gp": 0, "gq": 4, "gap": 1008, "lf": [("a", 0, 4), ("v", 4, 8)]}

SCRATCH = {}
for _n, _c, _d in (
        ("K", [M_ + 16], "bfloat16"), ("H", [UW + 16], "bfloat16"), ("HL HR TX", [XW], "bfloat16"), ("hs gL gR Tf Lf", [M_], "bfloat16"),
        ("nU VL VR St", [1792], "bfloat16"), ("Tg Mc", [1024], "bfloat16"), ("P0 P1 XB LF", [256], "bfloat16"),
        ("P2 Qb Mb", [512], "bfloat16"), ("Qi Qm", [512], "int32"),
        ("win0 win1 win2 win3", [WW], "bfloat16"), ("KL KR Wi Li Ri", [128], "int32"), ("SA SB Cs", [16], "int32"), ("Di", [64], "int32"),
        ("xF", [160], "float32"), ("X8 vf ls r0", [128], "float32"), ("dd", [136], "float32"), ("lf", [128], "bfloat16"), ("MX", [276, 8], "bfloat16"),
        ("TI", [8, 32], "float32"),
        ("TO", [256], "float32"), ("lown", [384], "uint16"), ("lin", [512], "uint16"), ("XO UO", [KX], "uint16"), ("AB off", [64], "uint16"), ("D3", [48], "uint16"),
        ("lo8", [8], "uint16"), ("FA", [128], "uint16"), ("ci", [8], "int32"), ("cf O8 KB", [8], "float32"), ("cc", [64], "float32"),
        ("O4 Or", [4], "float32"), ("O16 ta tb tc", [16], "float32"), ("Ci ai bi", [64], "int32"),
        ("BK WC WR WN Zs", [144], "bfloat16"), ("Cm Idn Blk2 Tri2 TriL Rst2 RstL WM ga gb", [128], "bfloat16"),
        ("J0 JC JD mn mx T1 df dg al oa ob oz", [64], "float32"), ("kk", [2, 66], "bfloat16"),
        ("S T2 dT", [72], "float32"), ("dead", [64], "bfloat16")):
    for _x in _n.split():
        SCRATCH[_x] = ("sbuf", [128] + _c, _d)
for _x in ("pA", "pB", "pC", "pD"):
    SCRATCH[_x] = ("psum", [128, 2, 512], "float32")
SEMAPHORES = ["sv", "sa_", "sp", "sg", "lhs", "lkl", "lkr", "lsa", "lsb", "lsw", "lhl", "outs", "sent",
              "arr0", "arr1", "arr2", "arr3", "far0", "far1", "far2", "far3"]
MSGS = ((0, 4), (1, 8), (2, 8), (3, 4))
MXO = {"Y": 0, "G": 64, "Ihi": 128, "Ilo": 146, "W3o": 164, "W3f": 180, "WT": 196, "WU": 212, "WS": 228, "WCL": 244, "WCR": 260}


def helpers_of(T, topo, q):
    n = len(T.cores)
    src = T.cores[q]
    dsts = [T.cores[(q - d) % n] for d in range(1, FAR + 1)]
    ok = [c for c in topo.cores_of(src) if c != src and all(topo.may_write(c, x) for x in dsts)]
    near = [c for c in ok if topo.die(c) == topo.die(src)]
    other = [c for c in ok if topo.die(c) != topo.die(src)]
    return [near[0], other[0], near[1], other[1]], dsts


def bits(engs):
    m = 0
    for e in engs:
        m |= 1 << e
    return m


def dst_id(topo, dst, src):
    rid, pid = topo.addr(dst, src)
    return DstId(rid=rid, pnc=pid)


def stage(T, m):
    return T.lown[:, 0:256] if m == 1 else T.gL[:, 512 * m:512 * m + 512]


def helper_program(g, core, T, topo):
    for q in range(len(T.cores)):
        hs_, dsts = helpers_of(T, topo, q)
        if core not in hs_:
            continue
        i = hs_.index(core)
        w = M_ // len(hs_)
        sent = 0
        for m, n in MSGS:
            if m == 1 and i != 0:
                continue
            g.wait_ge(T.sem["arr%d" % m], n)
            tr = []
            for d, x in enumerate(dsts):
                c0 = d * M_ + i * w
                dst = (T.H[:, c0:c0 + w], T.lin[:, 128 * d:128 * d + 128], T.TX[:, M_ + c0:M_ + c0 + w], T.HL[:, M_ + c0:M_ + c0 + w])[m]
                src = T.lown[:, 128 * d:128 * d + 128] if m == 1 else stage(T, m)
                tr.append(RemoteDMATransfer(dst_ids=[dst_id(topo, x, core)], dma_engine_mask=bits(topo.engines(core, x)[4 * d:4 * d + 4]),
                                            remote_sem=T.sem["far%d" % m], src=src, dst=dst))
            g.remote_dma_fused(tr, local_sem=T.sem.sent)
            sent += 4 * len(dsts)
        g.wait_ge(T.sem.sent, sent)


def rank_program(g, core, T, topo):
    rank = T.rank_of(core)
    if rank is None:
        helper_program(g, core, T, topo)
        return
    Q = {"v": g.vector, "a": g.scalar, "p": g.tensor, "g": g, "s": g.sync}
    esem = {"v": "sv", "a": "sa_", "p": "sp", "g": "sg"}
    total = {}
    seen = {k: {} for k in Q}
    alone = [False]
    wr, rd = {}, {}

    def wait(q, tok):
        s, n = tok
        if n is None:
            n = total[s]
        if q == "p" and s == "sp":
            return
        if seen[q].get(s, 0) < n:
            Q[q].wait_ge(T.sem[s], n)
            seen[q][s] = n

    def before(q, R, W):
        for k in list(R) + list(W):
            if k in wr:
                wait(q, wr[k])
        for k in W:
            for t in rd.get(k, []):
                wait(q, t)
        for k in R:
            if k.startswith("p:"):
                for t in rd.get(k, []):
                    if t[0] != esem.get(q):
                        wait(q, t)

    def after(tok, R, W):
        for k in R:
            rd.setdefault(k, []).append(tok)
        for k in W:
            wr[k] = tok
            rd[k] = []

    def op(q, fn, R, W):
        before(q, R, W)
        s = esem[q]
        if q == "g" and s in total and (alone[0] or "XB" in R):
            wait(q, (s, None))
        if q == "g":
            alone[0] = "XB" in R
        fn().then_inc(T.sem[s], 1)
        total[s] = total.get(s, 0) + 1
        after((s, total[s]), R, W)

    def dma(q, out, in_, s, R, W):
        before(q, R, W)
        Q[q].dma_start(out, in_).then_inc(T.sem[s], 16)
        total[s] = total.get(s, 0) + 16
        after((s, None), R, W)

    def mm(items, R, W, start=True, stop=True):
        before("p", R, W)
        for i, (o, l, r) in enumerate(items):
            ins = g.tensor.matmul(o, l, r, start and i == 0, stop and i == len(items) - 1)
        ins.then_inc(T.sem.sp, 1)
        total["sp"] = total.get("sp", 0) + 1
        after(("sp", total["sp"]), R, W)

    V = g.vector

    def ts(out, in0, s1, s2, o0, o1, R, W):
        if s2 is None:
            op("v", lambda: V.tensor_scalar(out, in0, s1, None, o0), R, W)
        else:
            op("v", lambda: V.tensor_scalar(out, in0, s1, s2, o0, o1), R, W)

    def tt(out, a, b, o, R, W):
        op("v", lambda: V.tensor_tensor(out, a, b, o), R, W)

    def cp(out, a, R, W):
        op("v", lambda: V.tensor_copy(out, a), R, W)

    def ms(out, c, W):
        op("v", lambda: V.memset(out, c), [], W)

    def act(out, in_, R, W, f=AF.Identity, **kw):
        op("a", lambda: g.scalar.activation(out, in_, f, **kw), R, W)

    def fiota(out, pat, W, R=(), base=0, cm=0):
        op("g", lambda: g.iota(out, pat, base, cm, allow_small_or_imprecise_dtypes=True), R, W)

    def asel(out, in_, pat, cmp_, fill_, base, cm, R, W):
        op("g", lambda: g.affine_select(out, in_, pat, cmp_, fill_, base, cm), R, W)

    def sel(W_, s):
        return W_[:, 15 - s:143 - s]

    def xs(lo, n, step=1):
        return T.xF[:, 16 + lo:16 + lo + n * step:step]

    AND, SHR, SAR, EQ, MUL, ADD = A.bitwise_and, A.logical_shift_right, A.arith_shift_right, A.is_equal, A.mult, A.add
    hs_, dsts = helpers_of(T, topo, rank)
    nh = len(hs_)
    total["sent"] = 0

    def push(m, parts, R):
        ne = dict(MSGS)[m]
        before("g", R, [])
        g.remote_dma_fused([RemoteDMATransfer(dst_ids=[dst_id(topo, hs_[i], core)],
                                              dma_engine_mask=bits(topo.engines(core, hs_[i])[j % 2::2][ne * (j // 2):ne * (j // 2) + ne]),
                                              remote_sem=T.sem["arr%d" % m], src=src, dst=stage(T, m))
                            for j, (i, src) in enumerate(parts)], local_sem=T.sem.sent)
        total["sent"] += ne * len(parts)

    for m, key in enumerate(("Hf", "lin", "TXf", "HLf")):
        total["far%d" % m] = 4 * FAR * (1 if m == 1 else nh)
        wr[key] = ("far%d" % m, None)

    C = {}

    def lin(name, x, a, b=0.0):
        n = len([1 for z in C.values() if z[1].startswith("c_")])
        col = T.cc[:, n:n + 1]
        (xc, xk), R = C[x], []
        if isinstance(a, str):
            R.append(C[a][1])
            a = C[a][0]
        if isinstance(b, str):
            R.append(C[b][1])
            b = C[b][0]
        act(col, xc, [xk] + R, ["c_" + name], scale=a, bias=b)
        C[name] = (col, "c_" + name)

    def eqm(out, pat, pk, tgt, val, W):
        if val is None:
            ts(out, pat, C[tgt][0], None, EQ, None, [pk, C[tgt][1]], W)
        elif isinstance(val, str):
            ts(out, pat, C[tgt][0], C[val][0], EQ, MUL, [pk, C[tgt][1], C[val][1]], W)
        else:
            ts(out, pat, C[tgt][0], val, EQ, MUL, [pk, C[tgt][1]], W)

    def mx(name, lo=0):
        return T.MX[:, MXO[name] + lo:MXO[name] + lo + 16, :]

    def dist(d, pat, pk, tgt):
        act(d, pat, [pk, C[tgt][1]], ["dist"], f=AF.Abs, scale=-1.0, bias=C[tgt][0])

    def eqa(out, d, val, W):
        act(out, d, ["dist", C[val][1]], W, f=AF.Relu, scale=-1.0, bias=C[val][0])

    dma("s", T.KL[:], T.kl[:], "lkl", [], ["KL"])
    dma("a", T.hs[:, 0:M_], T.h[:], "lhs", [], ["hs"])
    dma("s", T.KR[:], T.kr[:], "lkr", [], ["KR"])
    dma("s", T.SA[:], T.sa[:], "lsa", [], ["SA"])
    dma("s", T.SB[:], T.sb[:], "lsb", [], ["SB"])
    dma("s", T.H[0::2, OWNU:UW], T.h[1::2, :], "lsw", [], ["Ho0"])
    dma("s", T.H[1::2, OWNU:UW], T.h[0::2, :], "lsw", [], ["Ho1"])

    op("g", lambda: g.iota(T.ci[:, 0:1], [[0, 1]], 0, 1), [], ["p"])
    fiota(T.xF[:], [[1, 160]], ["xF"], base=-16)
    fiota(T.X8[:], [[16, 8], [0, 2], [1, 8]], ["X8"])
    fiota(T.XB[:], [[1, 256]], ["XB"])
    fiota(T.XB[64:65, :], [[1, 8], [0, 32]], ["XB2"], ["XB"])
    p = T.ci[:, 0:1]
    ms(T.Zs[:, 0:3], 0.0, ["Zs0"])
    ms(T.Cm[0:65, :], 0.0, ["Cm"])
    for j, m_ in ((1, 15), (2, 7), (3, 16), (4, 8), (5, 112), (7, 3)):
        ts(T.ci[:, j:j + 1], p, m_, None, AND, None, ["p"], ["ci%d" % j])
    ts(T.ci[:, 6:7], p, 2, 3, SHR, AND, ["p"], ["ci6"])
    ms(T.MX[:, MXO["Ilo"], :], 0.0, ["Ilo0"])
    cp(T.cf[:], T.ci[:], ["p"] + ["ci%d" % j for j in range(1, 8)], ["cf"])
    for j, name in enumerate(("p", "k", "k8", "p16", "hi8", "g16", "r4", "i4")):
        C[name] = (T.cf[:, j:j + 1], "cf")
    ms(T.MX[:, MXO["WU"]:MXO["WS"] + 16, :], 0.0, ["WU", "WS"])
    lin("tY", "r4", 1.0, "g16")
    lin("lo0", "k8", 32.0, "p16")
    lin("vb", "k", 128.0, MM)
    lin("lo1", "hi8", 0.125, "lo0")
    eqm(T.O4[:], xs(0, 4), "xF", "i4", None, ["O4"])
    eqm(T.Or[:], xs(0, 4), "xF", "r4", None, ["Or"])
    eqm(T.O16[:], xs(0, 16), "xF", "k", None, ["O16"])
    eqm(T.O8[:], xs(0, 8), "xF", "k8", None, ["O8"])
    for j in range(4):
        C["i%d" % j] = (T.O4[:, j:j + 1], "O4")
        C["r%d" % j] = (T.Or[:, j:j + 1], "Or")
    for j in range(16):
        C["e%d" % j] = (T.O16[:, j:j + 1], "O16")
    for j in range(8):
        C["o%d" % j] = (T.O8[:, j:j + 1], "O8")
    ts(T.vf[:], xs(0, 128), C["vb"][0], None, ADD, None, ["xF", "c_vb"], ["vf"])
    ts(T.Zs[:, 3:131], T.X8[:], 4.0, C["g16"][0], A.subtract, EQ, ["X8", "cf"], ["Zs"])
    ts(T.lo8[:], xs(0, 8), 2.0, C["lo1"][0], MUL, ADD, ["xF", "c_lo1"], ["lo8"])
    eqm(T.Zs[:, 11:131:16], xs(0, 8, 16), "xF", "g16", None, ["Zs"])
    d_ = T.dd[:, 0:128]
    dist(d_, xs(0, 128), "xF", "tY")
    lin("tG", "tY", 1.0, 3.0)
    for j in range(4):
        eqa(mx("Y", 16 * j), d_, "i%d" % j, ["Y%d" % j])
    for c in (("qs0", "r2", 1.0 / 256 - 1, 1.0), ("qo0", "r2", -0.5 + 1.0 / 512), ("qt0", "r0", BIG - 1, 1.0), ("qu", "r3", -float(2 ** 20)),
              ("qs", "r3", 1.0 / 65536 - 1, "qs0"), ("qo", "r3", 16 - 0.5 + 1.0 / 131072, "qo0")):
        lin(*c)
    dist(d_, T.X8[:], "X8", "tG")
    for c in (("qt1", "r2", 255.0, "qt0"), ("kb", "e10", 8.0, "e1"), ("hi", "hi8", 0.125), ("t8", "hi8", -1.0, "p"), ("qt", "r3", 65535.0, "qt1")):
        lin(*c)
    for j in range(4):
        eqa(mx("G", 16 * j), d_, "i%d" % j, ["G%d" % j])
    lin("t3", "o3", 4.0, "t8")
    lin("lo", "hi", -1.0, 1.0)
    dist(T.dd[:], xs(0, 136), "xF", "p")
    act(T.KB[:], xs(0, 8), ["xF", "c_kb"], ["KB"], scale=C["kb"][0])
    eqa(T.MX[:, MXO["Ihi"]:MXO["Ihi"] + 17, :], T.dd[:], "hi", ["Ihi"])
    eqa(mx("Ilo", 1), d_, "lo", ["Ilo"])
    lin("bf0", "e7", -MM)
    dist(d_, T.X8[:], "X8", "t3")
    lin("bf", "e15", 1.0, "bf0")
    eqa(mx("W3f"), d_, "r2", ["W3f"])
    eqa(mx("W3o"), d_, "r0", ["W3o"])
    cols = [("bo0", "e15", -MM), ("e45", "o4", 1.0, "o5"), ("w0", "o1", 256.0, "o0"), ("bo", "e7", 1.0, "bo0"), ("u0", "o3", -1.0, "o6"),
            ("w1", "o2", 65536.0, "w0"), ("m4", "r0", 1.0, "r2"), ("u", "e45", 1.0, "u0"), ("w", "e45", -float(2 ** 24), "w1"),
            ("y8", "k8", -1.0, "p"), ("sd", "e1", 1.0 / 8192), ("wL", "w", "lo"), ("chF", "e45", -BIG, BIG), ("c2", "hi", 1.0, "g16"),
            ("wR", "w", "hi"), ("ch0", "o4", 1.0, "chF"), ("g32", "g16", 2.0), ("ch", "o5", 1.0, "ch0"), ("g2k", "g16", 128.0)]
    for q_, j, x in ((0, 0, 1.0), (64, 10, 1.0), (0, 9, 8.0), (64, 9, -256.0)):
        wr["Cm%d" % (q_ + j)] = wr["Cm"]
        ms(T.Cm[q_:q_ + 1, j:128:16], x, ["Cm%d" % (q_ + j)])
    ms(T.H[:, GAP:GAP + 16], -262144.0, ["Hp"])
    ms(T.K[:, M_:M_ + 16], 0.0, ["Kp"])

    push(0, [(i, T.hs[:, 512 * i:512 * i + 512]) for i in range(nh)], ["hs"])

    ts(T.lf[:], T.KL[:], 0.0, None, EQ, None, ["KL"], ["lf"])
    ts(T.r0[:], T.KR[:], 2048.0, None, MUL, None, ["KR"], ["r0"])
    tt(T.ls[:], T.lf[:], T.vf[:], MUL, ["lf", "vf"], ["ls"])
    mm([(T.pA[:, 0, :], T.Zs[:, 3 - i:131 - i], T.hs[:, 512 * i:512 * i + 512]) for i in range(4)], ["Zs0", "Zs", "hs"], ["p:A0"], stop=False)
    mm([(T.pA[:, 0, 128 * j:128 * j + 128], mx("Y", 16 * j), T.lf[:]) for j in range(4)], ["lf", "Y0", "Y1", "Y2", "Y3"], ["p:A0"], start=False)
    tt(T.r0[:], T.r0[:], T.KL[:], ADD, ["r0", "KL"], ["r0"])

    def digits(step, h):
        c = slice(256 * h, 256 * h + 256)
        if step == 0:
            ts(T.Qi[:, c], T.pA[:, 0, c], C["qs"][0], C["qo"][0], MUL, ADD, ["p:A0", "c_qs", "c_qo"], ["Qi%d" % h])
        elif step == 1:
            ts(T.Qm[:, c], T.Qi[:, c], 255, None, AND, None, ["Qi%d" % h], ["Qm%d" % h])
        else:
            ts(T.Qb[:, c], T.Qm[:, c], C["qt"][0], C["qu"][0], MUL, ADD, ["Qm%d" % h, "c_qt", "c_qu"], ["Qb%d" % h])

    digits(0, 0)
    digits(0, 1)
    tt(T.TI[:, :, 0:16], T.r0[:], T.ls[:], ADD, ["r0", "ls"], ["TI0"])
    digits(1, 0)
    digits(1, 1)
    act(T.TI[:, :, 16:32], T.TI[:, :, 0:16], ["TI0"], ["TI1"])
    digits(2, 0)
    digits(2, 1)
    banks = [(T.pB, 0, "p:B0"), (T.pB, 1, "p:B1"), (T.pC, 0, "p:C0"), (T.pC, 1, "p:C1")]
    for P_, b, key in banks:
        mm([(P_[:, b, 256 * h:256 * h + 256], T.Cm[0:65, :], T.XB[0:65, :]) for h in range(2)],
           ["Cm0", "Cm9", "Cm73", "Cm74", "XB", "XB2"], [key], stop=False)
    for i in range(4):
        P_, b, key = banks[i]
        mm([(P_[:, b, :], mx("G", 16 * i), T.Qb[:])], ["G%d" % i, "Qb0", "Qb1"], [key], start=False)
    op("v", lambda: V.transpose(T.TO[:], T.TI[:]), ["TI0", "TI1"], ["TO"])
    cp(T.Wi[:], T.TO[:].indirect(T.lo8[:]), ["TO", "lo8"], ["Wi"])
    ts(T.Ri[:], T.Wi[:], 11, None, SHR, None, ["Wi"], ["Ri"])
    ts(T.Li[:], T.Wi[:], M_ - 1, None, AND, None, ["Wi"], ["Li"])
    ts(T.lown[:, 128:256], T.Ri[:], float(M_), None, A.min, None, ["Ri"], ["loR"])
    cp(T.lown[:, 256:384], T.Li[:], ["Li"], ["loL"])
    cp(T.lown[:, 0:128], T.Ri[:], ["Ri"], ["loQ"])
    push(1, [(0, T.lown[:, 0:256])], ["loR", "loQ"])
    for b8 in range(8):
        P_, b, key = banks[b8 // 2]
        src, out, kb = P_[:, b, 256 * (b8 % 2):256 * (b8 % 2) + 256], T.K[:, 256 * b8:256 * b8 + 256], T.KB[:, b8:b8 + 1]
        if OPT["kp"][b8 // 2] == "v":
            ts(out, src, kb, None, ADD, None, [key, "KB"], ["K%d" % b8])
        else:
            act(out, src, [key, "KB"], ["K%d" % b8], bias=kb)
    KA = ["K%d" % b for b in range(8)] + ["Kp"]

    tb = [(T.pD, 0, "p:D0"), (T.pD, 1, "p:D1"), (T.pA, 0, "p:A0"), (T.pA, 1, "p:A1")]

    def t_self(i, bank, W3):
        P_, b, key = bank
        mm([(P_[:, b, :], mx(W3), T.K[:, 512 * i:512 * i + 512])], ["K%d" % (2 * i), "K%d" % (2 * i + 1), W3], [key], stop=False)

    def t_mm(i, bank, W1, W2, R):
        P_, b, key = bank
        c = slice(512 * i, 512 * i + 512)
        mm([(P_[:, b, :], W1, T.gL[:, c]), (P_[:, b, :], W2, T.gR[:, c])], R + ["gL%d" % i, "gR%d" % i], [key], start=False)

    def t_pass(q, out, bank, bias, W):
        P_, b, key = bank
        if q == "v":
            ts(out, P_[:, b, :], -1.0, C[bias][0], MUL, ADD, [key, C[bias][1]], W)
        else:
            act(out, P_[:, b, :], [key, C[bias][1]], W, scale=-1.0, bias=C[bias][0])

    for i in range(4):
        t_self(i, tb[i], "W3f")
    for i in range(4):
        c = slice(512 * i, 512 * i + 512)
        act(T.gL[:, c], T.K[:].indirect(T.lown[:, 256 + 32 * i:288 + 32 * i]), KA + ["loL"], ["gL%d" % i], scale=-1.0)
        ts(T.gR[:, c], T.K[:].indirect(T.lown[:, 128 + 32 * i:160 + 32 * i]), -1.0, None, MUL, None, KA + ["loR"], ["gR%d" % i])
        t_self(i, banks[i], "W3o")
        t_mm(i, tb[i], mx("Ihi", 1), mx("Ihi"), ["Ihi"])
    for i in range(4):
        t_mm(i, banks[i], mx("Ilo", 1), mx("Ilo"), ["Ilo", "Ilo0"])
    for i in range(4):
        t_pass("av"[i % 2], T.Tf[:, 512 * i:512 * i + 512], tb[i], "bf", ["Tf%d" % i])
        if i % 2:
            push(2, [(j, T.Tf[:, 512 * j:512 * j + 512]) for j in (i - 1, i)], ["Tf%d" % (i - 1), "Tf%d" % i])
    for q_, a_, b_ in OPT["lf"]:
        (act if q_ == "a" else cp)(T.Lf[:, 256 * a_:256 * b_], T.hs[:].indirect(T.lown[:, 256 + 16 * a_:256 + 16 * b_]), ["hs", "loL"], ["Lf" + q_])
    push(3, [(i, T.Lf[:, 512 * i:512 * i + 512]) for i in range(nh)], ["Lfa", "Lfv"])
    dma("s", T.HL[0::2, 0:M_], T.Lf[1::2, :], "lhl", ["Lfa", "Lfv"], ["HLo0"])
    dma("s", T.HL[1::2, 0:M_], T.Lf[0::2, :], "lhl", ["Lfa", "Lfv"], ["HLo1"])
    fiota(T.H[:, GAP + 16:OWNU], [[0, OWNU - GAP - 16]], ["Hg"])
    fiota(T.ga[:], [[0, 128]], ["ga"], base=2)
    asel(T.gb[:], T.ga[:], [[-16, 8], [0, 16]], A.is_ge, 0.0, 0, 1, ["ga"], ["gb"])
    asel(T.Blk2[:], T.gb[:], [[16, 8], [0, 16]], A.is_ge, 0.0, 15, -1, ["gb"], ["Blk2"])
    asel(T.gb[:], T.Blk2[:], [[0, 8], [1, 16]], A.is_ge, 0.0, -8, 0, ["Blk2"], ["gb"])
    asel(T.Tri2[:], T.Blk2[:], [[1, 128]], A.is_gt, 0.0, 0, -1, ["Blk2"], ["Tri2"])
    fiota(T.ga[:], [[0, 128]], ["ga"], base=8192)
    asel(T.Idn[:], T.ga[:], [[1, 128]], A.is_equal, 0.0, 0, -1, ["ga"], ["Idn"])
    asel(T.TriL[:], T.Tri2[:], [[1, 128]], A.not_equal, -1.0, 0, -1, ["Tri2"], ["TriL"])
    asel(T.Rst2[:], T.Blk2[:], [[-1, 128]], A.is_ge, 0.0, 0, 1, ["Blk2"], ["Rst2"])
    asel(T.RstL[:], T.Rst2[:], [[1, 128]], A.not_equal, 3.0, 0, -1, ["Rst2"], ["RstL"])
    fiota(T.JC[:], [[32, 64]], ["JC"], cm=2)
    fiota(T.JD[:], [[16, 64]], ["JD"], base=DUMP, cm=1)
    fiota(T.J0[:], [[2, 64]], ["J0"], cm=128)
    wins = [T.win0, T.win1, T.win2, T.win3]
    for i, wn in enumerate(wins):
        fiota(wn[:, 0:WZ], [[0, WZ]], ["win%d" % i])

    ts(T.Di[:, 0:16], T.SB[:], 31, None, AND, None, ["SB"], ["Di0"])
    ts(T.Di[:, 16:32], T.SB[:], 5, None, SHR, None, ["SB"], ["Di1"])
    ts(T.Di[:, 32:48], T.SB[:], 15, None, AND, None, ["SB"], ["Di2"])
    ts(T.Di[:, 48:64], T.SB[:], 4, None, SHR, None, ["SB"], ["Di3"])
    cp(T.AB[:, 0:16], T.SA[:], ["SA"], ["AB0"])
    ts(T.D3[:, 0:16], T.Di[:, 0:16], 8.0, None, MUL, None, ["Di0"], ["D30"])
    ts(T.D3[:, 16:32], T.Di[:, 16:32], 64.0, None, ADD, None, ["Di1"], ["D31"])
    cp(T.AB[:, 32:64], T.Di[:, 32:64], ["Di2", "Di3"], ["AB2"])
    cp(T.AB[:, 16:32], T.SB[:], ["SB"], ["AB1"])

    ms(T.H[:, UW:UW + 16], -262144.0, ["Hq"])
    for c in cols:
        lin(*c)
    for i in range(4):
        t_pass(OPT["to"][i], T.TX[:, 512 * i:512 * i + 512], banks[i], "bo", ["TXo%d" % i])
    TO_ = ["TXo%d" % i for i in range(4)]
    HO = ["Ho0", "Ho1"]
    HA = HO + ["Hf", "Hg", "Hp", "Hq"]
    act(T.St[:, 0:512], T.XB[:].indirect(T.D3[:, 0:32]), ["XB", "XB2", "D30", "D31", "c_sd"], ["St0"], scale=C["sd"][0])
    act(T.St[:, 512:768], T.K[:].indirect(T.AB[:, 0:16]), KA + ["AB0"], ["St1"])
    act(T.St[:, 768:1024], T.O16[:].indirect(T.AB[:, 32:48]), ["O16", "AB2"], ["St2"])
    wu, ws, wt, U16 = MXO["WU"], MXO["WS"], MXO["WT"], T.X8[:, 0:128:8]
    eqm(T.BK[:], xs(-15, 144), "xF", "g16", 8192.0, ["BK"])
    eqm(T.MX[:, wu:wu + 16, 4], U16, "X8", "g16", None, ["WU"])
    eqm(T.MX[:, ws:ws + 16:2, 4], xs(0, 8, 16), "xF", "g16", None, ["WS"])
    eqm(T.tb[:], U16, "X8", "g16", "e7", ["tb"])
    eqm(T.MX[:, wu:wu + 16, 5], U16, "X8", "g16", -1.0, ["WU"])
    eqm(T.MX[:, ws:ws + 16:2, 3], xs(0, 8, 16), "xF", "g16", None, ["WS"])
    eqm(T.tc[:], U16, "X8", "g16", "e15", ["tc"])
    for name, m_, e_ in (("WCL", "r0", "e3"), ("WCR", "r2", "e11")):
        eqm(mx(name), T.X8[:], "X8", "t8", m_, [name])
    eqm(mx("WT"), xs(0, 128), "xF", "p", "m4", ["WT"])
    eqm(T.ta[:], xs(0, 16, 8), "xF", "y8", "u", ["ta"])
    for name, m_, e_ in (("WCL", "r0", "e3"), ("WCR", "r2", "e11")):
        ts(T.MX[:, MXO[name]:MXO[name] + 16, 4:6], T.MX[:, wu:wu + 16, 4:6], C[e_][0], None, MUL, None, ["WU", "O16"], [name])
    tt(T.MX[:, wt:wt + 16, 4], T.tb[:], T.ta[:], ADD, ["ta", "tb"], ["WT"])
    eqm(T.WC[:], xs(-15, 144), "xF", "g16", "wL", ["WC"])
    tt(T.MX[:, wt:wt + 16, 5], T.tc[:], T.ta[:], A.subtract, ["ta", "tc"], ["WT"])
    late = [[lambda: eqm(T.WN[:], xs(-15, 144), "xF", "c2", "w", ["WN"]),
             lambda: eqm(T.WR[:], xs(-15, 144), "xF", "g16", "wR", ["WR"]),
             lambda: ms(T.kk[:, :, 0:66:65], 0.0, ["kk0"]),
             lambda: ms(T.T2[:, 0:66:65], 0.0, ["T20"])],
            [lambda: ts(T.WM[:], T.gb[:], -float(2 ** 24), None, MUL, None, ["gb"], ["WM"])]]

    def kid(q, i, n):
        t, c = i // 8, 16 * (i % 8)
        if t == 0:
            win, lst, R = T.H[:, OWNU:UW + 16], T.lown[:, 128 + c:128 + c + 16 * n], HO + ["Hq", "loR"]
        else:
            c += 128 * (t - 1)
            win, lst, R = T.H[:, M_ * (t - 1):GAP + 16], T.lin[:, c:c + 16 * n], ["Hf", "Hp", "lin"]
        (act if q == "a" else cp)(T.HR[:, 256 * i:256 * (i + n)], win.indirect(lst), R, ["HR%d" % j for j in range(i, i + n)])

    done = [0]

    def fill(na, nv):
        for q, n in (("a", na), ("v", nv)):
            while n and done[0] < 24:
                m = min(n, 8 - done[0] % 8)
                kid(q, done[0], m)
                done[0] += m
                n -= m

    TA = TO_ + ["TXf"]
    HLA = ["HLo0", "HLo1", "HLf"]
    HRA = ["HR%d" % i for i in range(24)]
    f = OPT["f"]

    def decode(k, c0):
        cp(T.Ci[:, 0:k], T.pD[:, 0, 0:k], ["p:D0"], ["Ci"])
        ts(T.ai[:, 0:k], T.Ci[:, 0:k], M_ - 1, None, AND, None, ["Ci"], ["ai"])
        ts(T.bi[:, 0:k], T.Ci[:, 0:k], 11, None, SAR, None, ["Ci"], ["bi"])
        tt(T.mn[:, 0:k], T.ai[:, 0:k], T.bi[:, 0:k], A.min, ["ai", "bi"], ["mn"])
        ts(T.UO[:, c0:c0 + k], T.mn[:, 0:k], float(OWNU), None, ADD, None, ["mn"], ["U%d" % c0])
        tt(T.mx[:, 0:k], T.ai[:, 0:k], T.bi[:, 0:k], A.max, ["ai", "bi"], ["mx"])
        cp(T.XO[:, c0:c0 + k], T.mx[:, 0:k], ["mx"], ["X%d" % c0])

    def clamp(out, src, chi, R, W):
        ts(out, src, 0.0, C[chi][0], A.max, A.min, R + [C[chi][1]], W)

    fill(f[0], 8 - f[0])
    o = T.pA[:, 0, 0:256]
    mm([(o, sel(T.BK, 1 + e), T.St[:, 256 * e:256 * e + 256]) for e in range(2)] + [(o, mx("WT"), T.St[:, 512:768]), (o, mx("WU"), T.St[:, 768:1024])],
       ["BK", "WT", "WU", "St0", "St1", "St2"], ["p:A0"], stop=False)
    for f_ in late[0]:
        f_()
    act(T.St[:, 1280:1536], T.H[:, 0:GAP].indirect(T.AB[:, 16:32]), ["Hf", "AB1"], ["St3"], scale=-1.0)
    mm([(o, mx("WU"), T.St[:, 1280:1536])], ["St3"], ["p:A0"], start=False, stop=False)
    ts(T.LF[:], T.lin[:, 0:256], float(M_), BIG, A.is_ge, MUL, ["lin"], ["LF"])
    tt(T.St[:, 1536:1792], T.LF[:].indirect(T.AB[:, 48:64]), T.St[:, 768:1024], MUL, ["LF", "AB2", "St2"], ["St4"])
    mm([(o, mx("WS"), T.St[:, 1536:1792])], ["WS", "St4"], ["p:A0"], start=False)
    fill(f[1], f[2])
    clamp(T.P0[:], o, "ch0", ["p:A0"], ["P0"])
    mm([(T.pD[:, 0, 0:16], sel(T.WC, s), T.P0[:, s:256:16]) for s in range(16)], ["WC", "P0"], ["p:D0"])
    mm([(o, mx("WCL"), T.P0[:])], ["WCL", "P0"], ["p:A0"], stop=False)
    fill(0, f[3])
    decode(16, 0)

    act(T.nU[:, 1024:1280], T.H[:].indirect(T.UO[:, 0:16]), HA + ["U0"], ["nUa"], scale=-1.0)
    cp(T.Tg[:, 0:256], T.TX[:].indirect(T.XO[:, 0:16]), TA + ["X0"], ["Tg0"])
    mm([(o, mx("WU"), T.nU[:, 1024:1280])], ["nUa"], ["p:A0"], start=False, stop=False)
    mm([(o, mx("WT"), T.Tg[:, 0:256])], ["WT", "Tg0"], ["p:A0"], start=False)
    VE = (T.VL, T.VR)

    def early(at):
        for e, a_, b_ in OPT["early"][at]:
            lo, hi = 1024 + 256 * a_, 1024 + 256 * b_
            tt(VE[e][:, lo:hi], (T.HL, T.HR)[e][:].indirect(T.XO[:, 16 * a_:16 * b_]), T.nU[:, lo:hi], A.is_lt,
               (HLA, HRA)[e] + ["X0", "nUa"] + (["X16", "nUb"] if b_ > 1 else []), ["Ve%d%d" % (e, j) for j in range(a_, b_)])

    fill(f[4], f[5])
    early(0)
    clamp(T.P1[:], o, "ch", ["p:A0"], ["P1"])
    mm([(T.pD[:, 0, 0:32], sel(T.WN, 2 * q_), T.P1[:, q_:256:8]) for q_ in range(8)], ["WN", "P1"], ["p:D0"])
    WE = (mx("WCL"), mx("WCR"))
    for e in range(2):
        mm([(T.pA[:, e, 0:256], WE[e], T.P1[:])], ["WCL", "WCR", "P1"], ["p:A%d" % e], stop=False)
    for f_ in late[1]:
        f_()
    decode(32, 16)
    act(T.nU[:, 1280:1792], T.H[:].indirect(T.UO[:, 16:48]), HA + ["U16"], ["nUb"], scale=-1.0)
    cp(T.Tg[:, 0:512], T.TX[:].indirect(T.XO[:, 16:48]), TA + ["X16"], ["Tg0"])
    for e in range(2):
        mm([(T.pA[:, e, 0:256], mx("WU"), T.nU[:, 1280 + e:1792:2])], ["nUb"], ["p:A%d" % e], start=False, stop=False)
    for e in range(2):
        mm([(T.pA[:, e, 0:256], mx("WT"), T.Tg[:, e:512:2])], ["Tg0"], ["p:A%d" % e], start=False)
    fill(f[6], f[7])
    early(1)
    for e in range(2):
        clamp(T.P2[:, e:512:2], T.pA[:, e, 0:256], "ch", ["p:A%d" % e], ["P2%d" % e])
    mm([(T.pD[:, 0, 0:64], sel(T.WN, 2 * q_), T.P2[:, q_:512:8]) for q_ in range(8)], ["WN", "P20", "P21"], ["p:D0"])
    for e in range(2):
        mm([(T.pA[:, e, :], WE[e], T.P2[:])], ["P20", "P21"], ["p:A%d" % e], stop=False)
    fill(f[8], f[9])
    early(2)
    decode(64, 48)
    fill(f[10], f[11])
    early(3)

    cuts = OPT["cuts"]
    nc = len(cuts) - 1
    VLK, VRK, NU = ["VL%d" % i for i in range(nc)], ["VR%d" % i for i in range(nc)], ["nU%d" % i for i in range(nc)]
    for r in range(4):
        last = r == 3
        c0 = 48 + 64 * r
        xk, uk = "X%d" % c0, "U%d" % c0
        wn, wk = wins[r], "win%d" % r
        part = (lambda t, h: t[:, h:1024:2]) if r == 0 else (lambda t, h: t[:, 512 * h:512 * h + 512])
        for i in range(nc):
            a_, b_ = cuts[i], cuts[i + 1]
            act(T.nU[:, 16 * a_:16 * b_], T.H[:].indirect(T.UO[:, c0 + a_:c0 + b_]), HA + [uk], ["nU%d" % i], scale=-1.0)
        for h in range(2):
            act(T.Tg[:, 512 * h:512 * h + 512], T.TX[:].indirect(T.XO[:, c0 + 32 * h:c0 + 32 * h + 32]), TA + [xk], ["Tg%d" % h])

        def failed(e):
            mm([(T.pC[:, 0, 0:64], sel(T.BK, 4 * q_ + 2 * e + u), VE[e][:, 1024 + q_:1280:4]) for q_ in range(4) for u in range(2)]
               + [(T.pC[:, 0, 0:64], sel(T.BK, 2 * q_ + e), VE[e][:, 1280 + q_:1792:8]) for q_ in range(8)],
               ["BK"] + ["Ve%d%d" % (e, j) for j in range(3)], ["p:C0"], start=e == 1, stop=e == 0)

        def test(e, i):
            a_, b_ = cuts[i], cuts[i + 1]
            tt(VE[e][:, 16 * a_:16 * b_], (T.HL, T.HR)[e][:].indirect(T.XO[:, c0 + a_:c0 + b_]), T.nU[:, 16 * a_:16 * b_], A.is_lt,
               (HLA, HRA)[e] + [xk, "nU%d" % i], [("VL%d", "VR%d")[e] % i])

        def pay(h, W_, src, keys, stop=False):
            keys = keys if r == 0 or h == 1 else keys[:-1]
            mm([(T.pA[:, h, :], T.WM[:] if W_ == "WM" else mx(W_), part(src, h))], [W_] + keys, ["p:A%d" % h], start=False, stop=stop)

        def count(e):
            mm([(T.pB[:, e, 0:64], T.Idn[:], T.dead[:])] + [(T.pB[:, e, 0:64], sel(T.BK, s), VE[e][:, s:1024:16]) for s in range(16)],
               ["Idn", "BK", "dead"] + (VLK, VRK)[e], ["p:B%d" % e])

        TG = ["Tg0", "Tg1"]
        if r == 0:
            failed(1)
            for i in range(nc):
                test(1, i)
            early(4)
            for W_, src, keys in (("WU", T.nU, NU), ("WM", T.VR, VRK)):
                for h in range(2):
                    pay(h, W_, src, keys)
            failed(0)
            test(0, 0)
            test(0, 1)
            cp(T.dead[:], T.pC[:, 0, 0:64], ["p:C0"], ["dead"])
            test(0, 2)
            pay(0, "WT", T.Tg, TG, True)
            pay(1, "WT", T.Tg, TG, True)
            count(1)
            count(0)
        else:
            for i in range(nc):
                test(1, i)
                test(0, i)
            pay(0, "WU", T.nU, NU)
            pay(0, "WM", T.VR, VRK)
            pay(1, "WU", T.nU, NU)
            pay(0, "WT", T.Tg, TG, True)
            pay(1, "WM", T.VR, VRK)
            count(1)
            pay(1, "WT", T.Tg, TG, True)
            count(0)
        chi = "chF" if last else "ch"

        def top(at):
            if OPT["c1"] == at:
                ts(part(T.Mc, 1), T.Mb[:], C[chi][0], None, A.min, None, ["Mb", C[chi][1]], ["Mc1"])

        act(T.Mb[:], T.pA[:, 1, :], ["p:A1"], ["Mb"], f=AF.Relu)
        clamp(part(T.Mc, 0), T.pA[:, 0, :], chi, ["p:A0"], ["Mc0"])
        tt(T.T1[:], T.pB[:, 1, 0:64], T.JD[:], A.min, ["p:B1", "JD"], ["T1"])
        top(0)
        ts(T.kk[:, :, 1:65], T.pB[:, :, 0:64], 0.0, None, EQ, None, ["p:B0", "p:B1"], ["kk"])
        mm([(T.pC[:, 1, 0:65], T[W_][:], T.kk[:, e, u:u + 65]) for W_, e, u in (("RstL", 0, 0), ("TriL", 0, 1), ("Rst2", 1, 0), ("Tri2", 1, 1))],
           ["RstL", "Rst2", "TriL", "Tri2", "kk", "kk0"], ["p:C1"])
        tt(T.T2[:, 1:65], T.pB[:, 0, 0:64], T.T1[:], A.min, ["p:B0", "T1"], ["T2"])
        top(1)
        tt(T.dT[:, 0:65], T.T2[:, 1:66], T.T2[:, 0:65], A.subtract, ["T2", "T20"], ["dT"])
        top(2)
        op("v", lambda: V.tensor_tensor_scan(T.S[:, 0:65], T.pC[:, 1, 0:65], T.dT[:, 0:65], 0.0, ADD, ADD), ["p:C1", "dT"], ["S"])
        top(3)
        ts(T.off[:], T.S[:, 0:64], 3.0, None, ADD, None, ["S"], ["off"])
        cp(wn[:].indirect(T.off[:]), T.Mc[:], ["off", "Mc0", "Mc1"], [wk])
        b = int(last)
        mm([(T.pD[:, b, 0:64], sel(T.WN if s < 15 else T.WC, s), wn[:, 2 + 2 * s:2019 + 2 * s:32]) for s in range(16)]
           + [(T.pD[:, b, 0:64], sel(T.WR, s), wn[:, 3 + 2 * s:2020 + 2 * s:32]) for s in range(16)]
           + [(T.pD[:, b, 0:64], sel(T.WR, 0), wn[:, 0:2017:32])], ["WN", "WC", "WR", wk], ["p:D%d" % b])
        if not last:
            ts(T.dead[:], T.JC[:], C["g32"][0], T.S[:, 64:65], A.subtract, A.is_ge, ["JC", "c_g32", "S"], ["dead"])
            for h in range(2):
                mm([(T.pA[:, h, :], WE[e], wn[:, 1024 * h + o_:1024 * h + o_ + 1023:2]) for e, o_ in ((0, 2), (1, 3), (1, 0))],
                   [wk], ["p:A%d" % h], stop=False)
            decode(64, c0 + 64)

    mm([(T.pD[:, 0, 0:64], sel(W_, s), wn[:, o_ + 128 * s:o_ + 128 * s + 127:2]) for s in range(16) for W_, o_ in ((T.WC, 2), (T.WR, 3), (T.WR, 0))],
       [wk], ["p:D0"])
    ts(T.df[:], T.J0[:], C["g2k"][0], T.S[:, 64:65], A.subtract, A.is_ge, ["J0", "c_g2k", "S"], ["df"])
    ts(T.al[:], T.df[:], -1.0 / 8192, 1.0 / 8192, MUL, ADD, ["df"], ["al"])
    ts(T.dg[:], T.df[:], 1.0 - M_, float(M_), MUL, ADD, ["df"], ["dg"])

    def split(b):
        cp(T.Ci[:], T.pD[:, b, 0:64], ["p:D%d" % b], ["Ci"])
        ts(T.ai[:], T.Ci[:], M_ - 1, None, AND, None, ["Ci"], ["ai"])
        ts(T.bi[:], T.Ci[:], 11, None, SHR, None, ["Ci"], ["bi"])

    split(1)
    ts(T.FA[:, 0:64], T.ai[:], float(OWNU), None, ADD, None, ["ai"], ["FA"])
    ts(T.FA[:, 64:128], T.bi[:], -float(M_), None, ADD, None, ["bi"], ["FB"])
    fc = OPT["fc"]
    for i, (q_, a_, b_) in enumerate(fc):
        (act if q_ == "a" else cp)(T.gL[:, 64 * a_:64 * b_], T.H[:].indirect(T.FA[:, 4 * a_:4 * b_]), HA + ["FA", "FB"][a_ // 16:(b_ + 15) // 16], ["fs%d" % i])
        mm([(T.pB[:, 0, 0:64], sel(T.BK, s % 16), T.gL[:, 64 * s:64 * s + 64]) for s in range(a_, b_)],
           ["BK", "fs%d" % i], ["p:B0"], start=i == 0, stop=i == len(fc) - 1)
    split(0)
    tt(T.oa[:], T.ai[:], T.df[:], A.subtract, ["ai", "df"], ["oa"])
    tt(T.ob[:], T.bi[:], T.dg[:], A.subtract, ["bi", "dg"], ["ob"])
    dma("s", T.ya[:], T.oa[:], "outs", ["oa"], [])
    dma("s", T.yb[:], T.ob[:], "outs", ["ob"], [])
    tt(T.oz[:], T.pB[:, 0, 0:64], T.al[:], MUL, ["p:B0", "al"], ["oz"])
    dma("a", T.ys[:], T.oz[:], "outs", ["oz"], [])
    for s in sorted(total, key=lambda s: s == "outs"):
        if max(seen[q].get(s, 0) for q in Q) < total[s]:
            g.wait_ge(T.sem[s], total[s])
